import numpy as np, ml_dtypes
CORES = [5,29,101,125,133,157,229,253]
N = 8
BF = ml_dtypes.bfloat16
W, Q, CAP, ST, RO = 4096, 256, 96, 4, 2
R = np.arange(16)[:, None]
def hashes(path, node, w):
    u = np.add.accumulate(path * w[..., 0:1], axis=-2); v = np.add.accumulate(path * w[..., 1:2], axis=-2)
    return (((u * v) >> 5) + 37 * node[..., None, :]) & (W - 1)
def begin(node, path):
    return {"L": node, "G": node, "F": node, "P": path, "X": path, "O": path, "done": np.zeros(node.shape, bool), "Z": np.zeros_like(path), "V": np.zeros_like(node)}
def step(A, nk, w, s):
    h = hashes(s["P"], s["L"], w)
    key = (np.take_along_axis(A, h.reshape(N, 8, 1, 16 * Q), 3) & 15).reshape(N, 8, 16, 16, Q)
    differ = (key != s["P"][:, :, :, None, :]) & (R <= R.T)[:, :, None]
    m = R + 1; match = np.sum(differ, axis=2) <= (m >> 2)
    best = np.max(np.where(match, m, 0), axis=2)
    at = np.take_along_axis(h, np.maximum(best - 1, 0)[:, :, None, :], 2)
    Z = np.take_along_axis(A, at, 3) >> 4; x = np.take_along_axis(nk, at[:, :, 0], 2); node, kind = x >> 2, x & 3
    live = ~s["done"]; hit = live & (best > 0); miss = live & (best == 0)
    plain, quoted, nodal, value = hit & (kind == 0), hit & (kind == 1), hit & (kind == 2), hit & (kind == 3)
    q_, m_ = quoted[:, :, None], miss[:, :, None]
    new = np.where(R < best[:, :, None], Z, np.where(q_, s["X"], s["P"]))
    return {"P": np.where((plain | quoted | nodal)[:, :, None], new, np.where(m_, s["X"], s["P"])), "X": np.where((quoted | nodal)[:, :, None], new, s["X"]), "O": s["O"],
            "L": np.where(plain | nodal, node, np.where(quoted | miss, s["G"], s["L"])), "G": np.where(nodal, node, s["G"]), "F": s["F"],
            "done": s["done"] | value, "Z": np.where(value[:, :, None], Z, s["Z"]), "V": np.where(value, node, s["V"])}
def finish(A, nk, w, s, t):
    place = hashes(s["O"], s["F"], w)[:, :, 15]; done = s["done"]; d_ = done[:, :, None]
    for a in range(N):
        for g in range(8):
            v = np.flatnonzero(done[a, g]); c, k = np.unique(place[a, g, v], return_index=True); v = v[k]
            A[a, g][:, c] = s["O"][a, g][:, v] + 16 * s["Z"][a, g][:, v]; nk[a, g, c] = 4 * s["V"][a, g, v] + 3
    O = np.where(d_, (s["O"] + s["Z"]) & 15, s["O"]); F = np.where(done, s["V"], s["F"])
    old = {"P": np.where(d_, O, s["P"]), "X": np.where(d_, O, s["X"]), "O": O, "L": np.where(done, F, s["L"]), "G": np.where(done, F, s["G"]), "F": F}
    new = begin(F, O)
    for x in "PXOLGF": new[x] = np.array(old[x])
    for a in range(N):
        q = (a - 1 - t) % N
        for g in range(8):
            mine = np.flatnonzero(~done[a, g])[:CAP]; come = np.flatnonzero(~done[q, g])[:CAP][:len(mine)]
            here, spare = mine[:len(come)], mine[len(come):]
            for x in "PXOLGF": new[x][a, g][..., here] = old[x][q, g][..., come]
            for x, y in (("P", "O"), ("X", "O"), ("L", "F"), ("G", "F")): new[x][a, g][..., spare] = old[y][a, g][..., spare]
    return new
def sym(rng, *shape):
    return np.where(rng.random(shape) < 0.7, rng.integers(0, 3, shape), rng.integers(0, 16, shape))
def start(rng):
    A = (sym(rng, N, 8, 16, W) + 16 * sym(rng, N, 8, 16, W)).astype(np.int32)
    nk = 4 * rng.integers(0, 1024, (N, 8, W)) + rng.choice(np.array([0, 0, 0, 1, 1, 2, 2, 3, 3, 3]), (N, 8, W))
    return A, nk, rng.integers(1, 18, (N, 8, 16, 2)), rng.integers(0, 1024, (N, 8, Q)), sym(rng, N, 8, 16, Q)
def plant(rng, A, nk, w, s, used, share, lens, vals, fam, edge):
    h = hashes(s["P"], s["L"], w)
    for a in range(N):
        for g in range(8):
            lane = np.flatnonzero(~s["done"][a, g] & (rng.random(Q) < share[a, g])); m = rng.choice(lens, lane.size); c = h[a, g, m - 1, lane]
            keep = ~used[a, g, c]; lane, m, c = lane[keep], m[keep], c[keep]; used[a, g, c] = True; n = lane.size
            low = R < m; r = np.where(low, rng.random((16, n)), 2.0); order = np.argsort(np.argsort(r, axis=0), axis=0)
            ch = (m >> 2) + rng.integers(0, 2, n) if edge else (rng.random(n) * ((m >> 2) + 1)).astype(np.int64)
            p = s["P"][a, g][:, lane]; col = A[a, g][:, c]
            key = np.where(low, np.where(order < ch, (p + 1 + rng.integers(0, 15, (16, n))) & 15, p), col & 15)
            z = col >> 4; node = nk[a, g, c] >> 2; kind = np.where(rng.random(n) < vals, 3, nk[a, g, c] & 3)
            other = (lane + fam * rng.integers(0, Q // fam, n)) % Q if fam else rng.integers(0, Q, n)
            lead = (kind == 3) & (rng.random(n) < (0.9 if fam else 0.5)); O = s["O"][a, g]
            z = np.where(lead, (O[:, other] - O[:, lane]) & 15, z); node = np.where(lead, s["F"][a, g, other], node)
            A[a, g][:, c] = key + 16 * z; nk[a, g, c] = 4 * node + kind
def walk(rng, A, nk, w, qn, qp, share, lens, vals=0.0, fam=0, edge=False, used=None):
    s = begin(qn, qp); used = np.zeros((N, 8, W), bool) if used is None else used
    for k in range(ST):
        plant(rng, A, nk, w, s, used, share, lens, vals, fam, edge)
        if k < ST - 1: s = step(A, nk, w, s)
def pack(A, nk, w, qn, qp):
    return {"sen": A.reshape(N, 128, W).astype(np.float32).astype(BF), "nk": nk.astype(np.int32), "wt": np.ascontiguousarray(w.reshape(N, 128, 2)).astype(np.int32),
            "qn": qn.astype(np.int32), "qp": qp.reshape(N, 128, Q).astype(np.float32).astype(BF)}
def setup_inputs(rng):
    A, nk, w, qn, qp = start(rng)
    walk(rng, A, nk, w, qn, qp, rng.choice(np.array([0.3, 0.6, 0.9]), (N, 8)), np.arange(1, 17))
    return pack(A, nk, w, qn, qp)
def setup_inputs_alike(rng):
    A, nk, w, qn, qp = start(rng)
    for a in range(N):
        for g in range(8):
            o = rng.integers(0, 1 if g % 2 == 0 else 3, Q); qn[a, g] = qn[a, g, o]; qp[a, g] = qp[a, g][:, o]
            if g < 6:
                h = hashes(qp[a, g], qn[a, g], w[a, g])[15]; A[a, g][:, h] = qp[a, g] + 16 * (A[a, g][:, h] >> 4); nk[a, g, h] = 4 * (nk[a, g, h] >> 2) + (a + g) % 4
    J = Q // 8; O = rng.integers(0, 16, (N, 16, J)); F = rng.integers(0, 1024, (N, J)); Y = rng.integers(0, 16, (N, 16, J)); E = rng.integers(0, 1024, (N, J))
    for a in range(N):
        b = (a + 1) % N; o = rng.integers(0, J, Q); own = rng.permutation(Q) < Q // 2
        qp[a, 6] = np.where(own, O[a][:, o], O[b][:, o]); qn[a, 6] = np.where(own, F[a, o], F[b, o])
        for path, node, z, to, kind in ((O[b], F[b], Y[b], E[b], 2), (Y[b], E[b], Y[b], E[b], 2), (Y[a], E[a], rng.integers(0, 16, (16, J)), rng.integers(0, 1024, J), 3), (O[a], F[a], np.zeros_like(O[a]), F[a], 3)):
            c = hashes(path, node, w[a, 6])[15]; A[a, 6][:, c] = path + 16 * z; nk[a, 6, c] = 4 * to + kind
    return pack(A, nk, w, qn, qp)
def setup_inputs_ends(rng):
    A, nk, w, qn, qp = start(rng); w[:, 3] = 17; w[:, 4] = 1; used = np.zeros((N, 8, W), bool); used[:, :, 0] = True; used[:, :, W - 1] = True
    nk = np.where(rng.random(nk.shape) < 0.5, 4 * rng.choice(np.array([0, 1023]), nk.shape) + (nk & 3), nk)
    qn = np.where(rng.random(qn.shape) < 0.3, rng.choice(np.array([0, 1023]), qn.shape), qn)
    i3 = np.indices((16, 16, 16)).reshape(3, -1); inv = pow(37, -1, W)
    qn[:, :, 0] = 0; qp[:, :, :, 0] = 0; qn[:, :, 1] = 1023; qp[:, :, :, 1] = 15
    qp[:, :, :, 2:10] = 0; qp[:, 3, :, 10:34] = 15
    for a in range(N):
        for g in range(8):
            A[a, g, :, 0] = 16 * rng.integers(0, 16, 16); nk[a, g, 0] = 4 * (nk[a, g, 0] >> 2) + (a + g) % 4
            z = 1 + rng.permutation(64)[:8]; c = 37 * z; qn[a, g, 2:10] = z
            A[a, g][:, c] = 0; nk[a, g, c] = 4 * rng.integers(0, 1024, 8) + (np.arange(8) + a + g) % 4; used[a, g, c] = True
            if g == 3:
                qn[a, g, 10:34] = rng.permutation(np.arange(1000, 1024)); c = hashes(qp[a, g], qn[a, g], w[a, g])[15, 10:34]
                A[a, g][:, c] = 15 + 16 * rng.integers(0, 16, (16, 24)); nk[a, g, c] = 4 * rng.integers(0, 1024, 24) + 2 + np.arange(24) % 2; used[a, g, c] = True
            u = np.sum(w[a, g, :3, 0:1] * i3, axis=0); v = np.sum(w[a, g, :3, 1:2] * i3, axis=0)
            node = ((W - 1 - ((u * v) >> 5)) * inv) & (W - 1); ok = np.flatnonzero(node < 1024)
            if ok.size:
                k = rng.choice(ok); qp[a, g, :, Q - 1] = 0; qp[a, g, :3, Q - 1] = i3[:, k]; qn[a, g, Q - 1] = node[k]
                A[a, g, :, W - 1] = qp[a, g, :, Q - 1] + 16 * rng.integers(0, 16, 16); nk[a, g, W - 1] = 4 * (nk[a, g, W - 1] >> 2) + (a + g + 1) % 4
    walk(rng, A, nk, w, qn, qp, np.full((N, 8), 0.9), np.array([1, 3, 4, 7, 8, 11, 12, 15, 16]), edge=True, used=used)
    return pack(A, nk, w, qn, qp)
def setup_inputs_room(rng):
    A, nk, w, qn, qp = start(rng); few = rng.random(A.shape) < 0.7
    A = (np.where(few, rng.integers(0, 3, A.shape), rng.integers(0, 8, A.shape)) + 16 * rng.integers(0, 8, A.shape)).astype(np.int32)
    nk = 4 * (nk >> 2) + rng.integers(0, 3, nk.shape); qp = np.where(rng.random(qp.shape) < 0.7, rng.integers(0, 3, qp.shape), rng.integers(0, 8, qp.shape))
    want = rng.choice(np.array([0, 1, CAP - 1, CAP, CAP + 1, Q - 256, Q]), (N, 8)); want[0] = (CAP, CAP + 1, Q, CAP - 1, 1, 0, CAP, CAP); want[1] = (CAP, CAP, 0, CAP + 1, Q, CAP, 1, CAP - 1)
    want[2, 3] = Q - 256; want[2, 5] = 0
    for a in range(N):
        for g in range(8):
            n = Q - int(want[a, g])
            if n == 0: continue
            w[a, g] = rng.integers(5, 18, (1, 2))
            p = rng.integers(8, 16, (16, 4 * Q)); i = rng.integers(0, 15, 4 * Q)
            p[i, np.arange(4 * Q)] = 8 + (p[15] + rng.integers(1, 8, 4 * Q)) % 8; node = rng.integers(0, 1024, 4 * Q); h = hashes(p, node, w[a, g])
            k = np.unique(h[14], return_index=True)[1]; k = k[np.unique(h[15, k], return_index=True)[1]]
            k = np.resize(rng.permutation(k), n); up = rng.permutation(Q)[:n]; c = h[14, k]
            z = np.zeros((16, n), np.int64); gap = p[i[k], k] - p[15, k]; z[15] = gap & 15; z[i[k], np.arange(n)] = (-gap) & 15
            qp[a, g][:, up] = p[:, k]; qn[a, g, up] = node[k]; A[a, g][:, c] = p[:, k] + 16 * z; nk[a, g, c] = 4 * node[k] + 3
    return pack(A, nk, w, qn, qp)
def setup_inputs_spread(rng):
    A, nk, w, qn, qp = start(rng); A = rng.integers(0, 256, A.shape).astype(np.int32); nk = rng.integers(0, 4096, nk.shape)
    w = np.minimum(np.exp2(4.2 * rng.random(w.shape)).astype(np.int64), 17); qn = np.minimum(np.exp2(10 * rng.random(qn.shape)).astype(np.int64) - 1, 1023)
    qp = np.minimum((np.exp2(4.5 * rng.random((N, 8, 1, Q))) * rng.random(qp.shape)).astype(np.int64), 15)
    walk(rng, A, nk, w, qn, qp, np.full((N, 8), 0.7), np.arange(1, 17))
    return pack(A, nk, w, qn, qp)
def setup_inputs_ties(rng):
    A, nk, w, qn, qp = start(rng); fam = Q // 16; w = np.ascontiguousarray(np.broadcast_to(rng.integers(1, 18, (N, 8, 1, 2)), w.shape))
    qn = np.tile(rng.integers(0, 1024, (N, 8, fam)), (1, 1, 16)); base = np.tile(rng.integers(0, 16, (N, 8, 16, fam)), (1, 1, 1, 16))
    i = rng.integers(0, 16, (N, 8, 1, Q)); j = (i + 1 + rng.integers(0, 15, i.shape)) % 16
    qp = np.take_along_axis(base, np.where(R == i, j, np.where(R == j, i, R)), 2)
    walk(rng, A, nk, w, qn, qp, np.full((N, 8), 0.9), np.arange(4, 16), vals=0.8, fam=fam)
    o = np.arange(Q).reshape(16, fam).T.reshape(-1); qn[:, 1::2] = qn[:, 1::2][..., o]; qp[:, 1::2] = qp[:, 1::2][..., o]
    return pack(A, nk, w, qn, qp)
def check_inputs(d):
    bad = []
    for k, hi, lo in (("sen", 255, 0), ("nk", 4095, 0), ("wt", 17, 1), ("qn", 1023, 0), ("qp", 15, 0)):
        x = np.asarray(d[k]).astype(np.float64)
        if not (np.all(x >= lo) and np.all(x <= hi) and np.all(x == np.floor(x))): bad.append("range of " + k)
    return bad
def reference(sen, nk, wt, qn, qp):
    A = sen.astype(np.float32).astype(np.int32).reshape(N, 8, 16, W); kn = nk.astype(np.int64); w = wt.astype(np.int64).reshape(N, 8, 16, 2)
    s = begin(qn.astype(np.int64), qp.astype(np.float32).astype(np.int64).reshape(N, 8, 16, Q))
    for t in range(RO):
        for k in range(ST): s = step(A, kn, w, s)
        s = finish(A, kn, w, s, t)
    return {"yp": np.concatenate([s["P"], s["X"]], axis=3).reshape(N, 128, 2 * Q).astype(np.float32).astype(BF), "yn": np.concatenate([s["L"], s["G"]], axis=2).astype(np.float32)}

@@ -1,0 +1,738 @@
+from concourse.mybir import AluOpType, AxisListType, ActivationFunctionType
+
+ALU = AluOpType
+ACT = ActivationFunctionType
+W, Q, CAP, ST, RO = 4096, 256, 96, 4, 2
+TB = 16
+TW = TB + W + 64
+LB = 64
+NB = Q // LB
+NKG, NNQ = 3, 2
+ARR, AW = 2048, 384
+BF, F32, I32, U16, F16 = "bfloat16", "float32", "int32", "uint16", "float16"
+CFG = {"gcyc": 1.5, "pe": 0.5, "hop": 100.0, "self": 60.0, "pace": 1.1, "slack": 40.0, "seed": 16, "noise": 100.0,
+       "vg": {(0, 0): 32}, "na": 3, "pc": 2,
+       "e": {("snd", 1, 0): "s", ("snd", 0, 3): "s", ("snd", 1, 1): "v", ("asm", 0): "v", ("asm", 32): "v",
+             ("fg", 0): "s", ("fg", 3): "s"}}
+
+SB = {
+    "ft": (TW, BF), "zt": (TW, BF), "kt": (TW, BF),
+    "bw0": (ARR + AW, BF), "bw1": (ARR + AW, BF), "outb": (768, BF), "pb": (256, BF),
+    "snd0": (AW, BF), "snd1": (AW, BF), "cout0": (8, BF), "cout1": (8, BF), "cin0": (8, BF), "cin1": (8, BF),
+    "wti": (2, I32), "wtf": (2, F32), "nkc": (256, I32), "nki": (512, I32), "fc": (1280, BF),
+    "qni": (256, I32), "qnh": (256, BF), "qnf": (256, F16), "g8": (256, BF), "ones": (128, BF), "zero": (144, BF),
+    "iop": (4, I32), "col": (32, F32), "io16": (16, F32), "xio": (128, BF), "ee": (16, F32), "rm": (16, F32), "gm": (8, F32),
+    "mx": (128 * 18, BF), "st4": (144, BF), "st15": (144, BF), "tg": (32, F32), "pt5": (64, BF),
+    "f1": (896, BF), "f2": (896, BF), "f3": (896, BF), "f4": (1152, BF), "f5": (512, BF),
+    "yw": (16, BF), "kb": (8, F32), "lt4": (64, F32), "dmy": (16, F32), "tri": (256, BF), "dbig": (128, BF),
+    "usb": (256, F32), "tt": (256, F32), "xi": (256, I32), "hi": (256, I32), "off": (256, U16),
+    "hs": (256, F16), "hs0": (256, F16), "mat": (256, BF), "ohh": (256, F16), "mm": (256, BF), "sc": (256, F32),
+    "off2": (64, U16), "fg": (1024, BF), "tz": (256, BF), "eb": (256, BF),
+    "ncb": (512, BF), "junk": (256, BF), "junk2": (256, BF), "cn": (24, F32), "lst": (8, U16),
+    "atw": (64, F32), "cod": (64, F32), "cod2": (32, F32), "codi": (32, I32), "atv": (16, U16),
+    "zz": (256, BF), "zraw": (256, BF), "fv": (256, BF), "tb": (256, BF),
+    "prow": (256, F16), "plt": (16, F32), "pls": (16, F32), "pld": (16, F32), "eqb": (1024, BF), "win": (256, BF),
+    "so1": (16, F32), "so2": (16, F32), "sof": (16, U16),
+    "nct": (32, F32), "lv": (16, F32), "cux": (32, F32), "oa": (64, F32), "ob": (64, F32), "o0": (64, F32),
+    "ca": (64, F32), "cx": (64, F32), "aa": (64, F32), "ab": (64, F32), "aof": (64, U16), "yno": (512, F32),
+}
+for _k in range(NKG):
+    SB["kg%d" % _k] = (16 * LB, BF)
+for _k in range(NNQ):
+    SB["nq%d" % _k] = (9 * LB, BF)
+SCRATCH = {k: ("sbuf", [128, v[0]], v[1]) for k, v in SB.items()}
+for _k in range(8):
+    SCRATCH["ps%d" % _k] = ("psum", [128, 512], F32)
+SEMAPHORES = ["sv", "ss", "sp", "sg", "ls", "hl", "ar0", "ar1", "ar2", "ar3"] + ["d%d" % k for k in range(16)]
+TWO = (BF, U16, F16)
+
+
+def A(name, c0=0, c1=None, step=1, p0=0, p1=128, pstep=1):
+    if c1 is None:
+        c1 = 512 if name.startswith("ps") else SB[name][0]
+    return ("ap", name, c0, c1, step, p0, p1, pstep)
+
+
+def A8(name, c0, c1):
+    return A(name, c0, c1, 1, 0, 8)
+
+
+def C(name, c):
+    return A(name, c, c + 1)
+
+
+def IND(win, off):
+    return ("ind", win, off)
+
+
+def is_op(x):
+    return isinstance(x, tuple)
+
+
+def width(x):
+    if x[0] == "ind":
+        return 16 * width(x[2])
+    return (x[3] - x[2] + x[4] - 1) // x[4]
+
+
+def two_byte(x):
+    return x[0] == "ap" and not x[1].startswith("ps") and SB[x[1]][1] in TWO
+
+
+def regions(x):
+    if not is_op(x) or x[0] == "ext":
+        return []
+    if x[0] == "ind":
+        return regions(x[1]) + regions(x[2])
+    return [(x[1], x[2], x[3])]
+
+
+def real(T, x):
+    if not is_op(x):
+        return x
+    if x[0] == "ind":
+        return real(T, x[1]).indirect(real(T, x[2]))
+    if x[0] == "ext":
+        return T[x[1]][x[2]]
+    rows = slice(x[5], x[6], x[7]) if x[7] != 1 else slice(x[5], x[6])
+    cols = slice(x[2], x[3], x[4]) if x[4] != 1 else slice(x[2], x[3])
+    return T[x[1]][rows, cols]
+
+
+def build_ops():
+    ops = []
+    gc_ = CFG["gcyc"]
+
+    def add(eng, kind, args, outs, ins, cost, lat=0.0):
+        wr, rd = [], []
+        for o in outs:
+            if o[0] == "ind":
+                wr += regions(o[1])
+                rd += regions(o[2])
+            else:
+                wr += regions(o)
+        for i in ins:
+            rd += regions(i)
+        ops.append({"eng": eng, "kind": kind, "args": args, "wr": wr, "rd": rd, "cost": cost, "lat": lat})
+
+    def vcost(out, ins, tt=False):
+        if out[0] == "ind":
+            return 50 + 3.5 * width(out)
+        if ins and ins[0][0] == "ind":
+            return 50 + gc_ * width(out)
+        n = width(out)
+        if tt:
+            n = 2 * n if not any(i[1].startswith("ps") for i in ins) else n
+        elif two_byte(out) and all(two_byte(i) for i in ins):
+            n = n / 2
+        return max(64.0, n)
+
+    def ts(out, in0, s1, op0, s2=None, op1=None):
+        add("v", "ts", (out, in0, s1, s2, op0, op1), [out], [in0, s1, s2], vcost(out, [in0]))
+
+    def tt(out, in0, in1, op):
+        add("v", "tt", (out, in0, in1, op), [out], [in0, in1], vcost(out, [in0, in1], True))
+
+    def cp(out, in0):
+        add("v", "cp", (out, in0), [out], [in0], vcost(out, [in0]))
+
+    def ms(out, c):
+        add("v", "ms", (out, c), [out], [], vcost(out, []))
+
+    def scan(out, d0, d1, init, op0, op1):
+        add("v", "scan", (out, d0, d1, init, op0, op1), [out], [d0, d1, init], float(width(out)))
+
+    def act(out, in0, func, bias=0.0, scale=1.0, accum=None):
+        n = 65 + gc_ * width(out) if in0[0] == "ind" else max(64.0, width(out)) + 20
+        add("s", "act", (out, in0, func, bias, scale, accum), [out] + ([accum] if accum else []), [in0, bias, scale], n)
+
+    def copy(eng, out, in0):
+        if eng == "v":
+            cp(out, in0)
+        else:
+            act(out, in0, ACT.Copy)
+
+    def affine(out, in0, scale, bias=0.0):
+        act(out, in0, ACT.Identity, bias, scale)
+
+    def en(name, dflt="v"):
+        return CFG["e"].get(name, dflt)
+
+    def pe(*groups, start=True, stop=True):
+        outs, ins, cost, gs = [], [], 0.0, []
+        for out, terms in groups:
+            terms = [t if len(t) == 3 else (out, t[0], t[1]) for t in terms]
+            gs.append(terms)
+            for o, l, r in terms:
+                outs.append(o)
+                ins += [l, r]
+                cost += CFG["pe"] * max(min(64, width(l)), width(r))
+        add("p", "mm", gs, outs, ins, cost, 60.0)
+        ops[-1]["ends"] = (start, stop)
+
+    def iota(out, pattern, base, cm):
+        add("g", "iota", (out, pattern, base, cm), [out], [], 150 + 2 * width(out))
+
+    def asel(out, in0, pattern, op, fill, base, cm):
+        add("g", "asel", (out, in0, pattern, op, fill, base, cm), [out], [in0], 190 + 2 * width(out))
+
+    ndma = [0]
+
+    def dma(q, out, in0, nbytes):
+        add(q, "dma", (out, in0, ndma[0]), [out], [in0], 60.0, 1800 + nbytes / 200.0)
+        ndma[0] += 1
+
+    def send(t, n, src, dst, lat):
+        add("g", "send", (t, n, src, dst), [], [src], 500.0)
+        add("x", "arrive", (n, len(ops) - 1), [dst], [], 0.0, lat)
+
+    def to_t(out, strip, src, lo, hi):
+        pe((out, [(A(strip, 15 - i, 143 - i), A(src, lo + i, hi, 16)) for i in range(16)]))
+
+    def M(k, name="mx"):
+        return A(name, 128 * k, 128 * k + 128)
+
+    IDM, NID, N16, JM, BON, UT, LT, WU, WV, PEN, SFX, LCM, K1R, K3R, Q16, DM, X16, R15 = [M(k) for k in range(18)]
+    SM, FM, VM, FFM = [A("f5", k, 512, 4) for k in range(4)]
+
+    def P5(m, j0, j1):
+        return A("pt5", j0 * 4 + m, (j1 - 1) * 4 + m + 1, 4)
+
+    (PC, GCOL, PF, QC, WP, YL, YG, LCW, THR, PH, SBI, VBI, T0, T1, T2, G7, P3, B0, T3) = [C("col", k) for k in range(19)]
+    C32, CM32 = 22, 24
+
+    def E(r, n=1):
+        return A("ee", r, r + n)
+
+    io, Z = A("io16"), A("zero", 0, 128)
+    blk = [[-16, 8], [0, 16]]
+
+    def row(out, in0, r, v):
+        asel(out, in0, blk, ALU.not_equal, v, -r, 1)
+
+    full = (slice(None), slice(None))
+    for k in range(4):
+        dma("y", A("ft", TB + 1024 * k, TB + 1024 * k + 1024), ("ext", "sen", (slice(None), slice(1024 * k, 1024 * k + 1024))), 262144 * (k + 1))
+    dma("s", A("bw0", 0, 256), ("ext", "qp", full), 65536)
+    dma("s", A8("qni", 0, 256), ("ext", "qn", full), 8192)
+    dma("s", A("wti"), ("ext", "wt", full), 1024)
+    dma("y", A("nkc"), ("ext", "nk", full), 1200000)
+
+    ms(A("ones"), 1.0)
+    iota(A("iop", 0, 1), [[0, 1]], 0, 1)
+    iota(io, [[1, 16]], 0, 0)
+    asel(IDM, A("ones"), [[1, 128]], ALU.is_equal, 0.0, 0, -1)
+    ms(A("zero"), 0.0)
+    affine(N16, IDM, -16.0)
+    asel(NID, Z, [[1, 128]], ALU.not_equal, -1.0, 0, -1)
+    asel(BON, A("ones"), blk, ALU.is_ge, 0.0, 0, 1)
+    asel(BON, BON, [[16, 8], [0, 16]], ALU.is_ge, 0.0, 15, -1)
+    asel(UT, BON, [[1, 128]], ALU.is_ge, 0.0, 0, -1)
+    asel(A8("g8", 128, 256), A8("ones", 0, 128), [[4, 8], [0, 4], [1, 4]], ALU.is_equal, 0.0, -1, -4)
+    asel(A8("g8", 0, 128), A8("ones", 0, 128), [[4, 8], [0, 4], [1, 4]], ALU.is_equal, 0.0, 0, -4)
+    asel(A8("g8", 0, 128), A8("g8", 0, 128), [[4, 8], [0, 4], [1, 4]], ALU.not_equal, -32.0, -1, -4)
+    asel(JM, A("ones"), [[-16, 8], [1, 16]], ALU.is_equal, 0.0, -15, 1)
+    iota(A("xio"), [[1, 128]], 0, 0)
+    asel(LT, BON, [[-1, 128]], ALU.is_ge, 0.0, 0, 1)
+    cp(PF, A("iop", 0, 1))
+    ts(A("iop", 1, 2), A("iop", 0, 1), 15, ALU.bitwise_and)
+    cp(PC, A("iop", 1, 2))
+    ts(GCOL, PF, PC, ALU.subtract, 0.0625, ALU.mult)
+    ts(A("gm"), A("io16", 0, 8), GCOL, ALU.is_equal)
+    ts(A("ee"), io, PC, ALU.is_equal)
+    ts(A("rm"), io, PC, ALU.is_ge)
+    ts(A("iop", 2, 3), A("iop", 0, 1), 2, ALU.arith_shift_right, 3, ALU.bitwise_and)
+    ts(A("iop", 3, 4), A("iop", 0, 1), 3, ALU.bitwise_and)
+    cp(QC, A("iop", 2, 3))
+    cp(P3, A("iop", 3, 4))
+    ts(T3, P3, 2.0, ALU.not_equal, P3, ALU.mult)
+    ts(WP, T3, 0.0, ALU.is_equal, 31.0, ALU.mult)
+    ts(WP, WP, 1.0, ALU.add)
+    ts(YL, QC, 0.0, ALU.is_equal, WP, ALU.mult)
+    ts(YG, QC, 1.0, ALU.is_equal, WP, ALU.mult)
+    ts(T0, E(10), -1310720.0, ALU.mult)
+    ts(LCW, YL, 1184.0, ALU.mult, T0, ALU.add)
+    affine(LCM, BON, LCW)
+    cp(A("wtf"), A("wti"))
+    affine(WU, UT, C("wtf", 0))
+    affine(WV, UT, C("wtf", 1))
+    ts(T1, P3, 0.0, ALU.is_equal, C("rm", 10), ALU.mult)
+    ts(VBI, T1, -192.0, ALU.mult, E(10), ALU.add)
+    ts(T2, P3, 1.0, ALU.is_equal, C("rm", 10), ALU.mult)
+    ts(B0, T2, 6144.0, ALU.mult, VBI, ALU.add)
+    ts(A8("qnh", 0, 256), A8("qni", 0, 256), 1.0 / 32, ALU.mult, 191.515625, ALU.add)
+    cp(A8("qnf", 0, 256), A8("qni", 0, 256))
+    pe((A("ps4", 0, 256), [(A8("g8", 0, 128), A8("qnh", 0, 256)), (A8("g8", 128, 256), A8("qnf", 0, 256))]))
+    affine(A("bw0", 768, 1024), A("ps4", 0, 256), C("rm", 10), B0)
+    act(A("bw0", 512, 768), A("bw0", 0, 256), ACT.Copy)
+    ms(A("bw0", 256, 512), 16.0)
+    for mi in range(7):
+        affine(M(mi, "f1"), IDM, C("rm", 8 + mi))
+        ts(M(mi, "f2"), JM, C("rm", 6 - mi), ALU.mult)
+    for lo, hi, bank in ((0, 512, "ps2"), (512, 896, "ps5")):
+        pe((A(bank, 0, hi - lo), [(IDM, A("f1", lo, hi)), (IDM, A("f2", lo, hi))]))
+        affine(A("f3", lo, hi), A(bank, 0, hi - lo), -1.0)
+    ts(G7, PF, PC, ALU.subtract, 7.0, ALU.add)
+    ts(A("tg", 0, 9), A("io16", 0, 9), 2.0, ALU.mult)
+    tt(A("tg", 0, 9), A("tg", 0, 9), A("rm", 7, 16), ALU.mult)
+    ts(A("tg", 16, 25), A("io16", 0, 9), -1.0, ALU.mult, G7, ALU.add)
+    tt(A("tg", 0, 9), A("tg", 0, 9), A("tg", 16, 25), ALU.add)
+    for mi in range(9):
+        ts(M(mi, "f4"), A("xio"), C("tg", mi), ALU.is_equal, C("rm", 7 if mi == 0 else 15), ALU.mult)
+    ts(THR, PC, 0.25, ALU.mult, 0.25, ALU.add)
+    affine(SFX, LT, -63.0)
+    affine(PEN, LT, -8192.0)
+    asel(PEN, PEN, [[1, 128]], ALU.not_equal, 8192.0, 0, -1)
+    iota(A("junk", 0, LB), [[0, LB // 16], [1, 16]], 0, 0)
+    ts(A("dbig", 0, LB), A("junk", 0, LB), PC, ALU.is_equal, 65536.0, ALU.mult)
+    ts(A("dbig", LB, 2 * LB), A("junk", 0, LB), PC, ALU.not_equal, 65536.0, ALU.mult)
+    row(K1R, Z, 2, 1.0)
+    row(Q16, Z, 11, -16.0)
+    row(DM, Z, 12, -32.0)
+    row(DM, DM, 13, 16.0)
+    row(K3R, Z, 4, 1.0)
+    row(R15, Z, 15, 1.0)
+    row(X16, Z, 12, 16.0)
+    ms(A("pt5"), 0.0)
+    tt(P5(0, 0, 2), E(4, 2), E(6, 2), ALU.add)
+    tt(P5(0, 4, 6), E(4, 2), E(6, 2), ALU.add)
+    cp(P5(0, 8, 10), E(8, 2))
+    ts(P5(0, 11, 12), E(12), -1.0, ALU.mult)
+    cp(P5(0, 13, 14), E(12))
+    ts(A("col", C32, C32 + 2), E(2, 2), 32.0, ALU.mult)
+    ts(A("col", CM32, CM32 + 2), E(2, 2), -32.0, ALU.mult)
+    ts(P5(1, 0, 2), E(0, 2), 0.0, ALU.mult, C("col", C32), ALU.add)
+    ts(P5(1, 2, 4), E(0, 2), C("col", CM32), ALU.add)
+    ts(P5(1, 4, 6), E(0, 2), 0.0, ALU.mult, C("col", CM32 + 1), ALU.add)
+    ts(P5(1, 6, 8), E(0, 2), C("col", C32 + 1), ALU.add)
+    cp(P5(1, 11, 12), E(2))
+    tt(P5(1, 12, 13), E(2), E(3), ALU.add)
+    for j in (0, 4, 8):
+        cp(P5(2, j, j + 2), E(0, 2))
+        cp(P5(3, j, j + (3 if j == 8 else 2)), E(8, 3 if j == 8 else 2))
+    for gi in range(8):
+        affine(A("f5", gi * 64, gi * 64 + 64), A("pt5"), C("gm", gi))
+    prev = E(10)
+    for n, (r, wv) in enumerate([(0, -32.0), (1, -32.0), (2, -192.0), (6, -224.0), (7, -32.0)]):
+        dst = SBI if n == 4 else C("col", 26 + n)
+        ts(dst, E(r), wv, ALU.mult, prev, ALU.add)
+        prev = dst
+
+    for k in range(8):
+        lo, hi = TB + 512 * k, TB + 512 * k + 512
+        bank = A("ps%d" % (0, 1, 3, 6, 7)[k % 5])
+        ts(A("zt", lo, hi), A("ft", lo, hi), 0.0625, ALU.mult, 191.53125, ALU.add)
+        pe((bank, [(IDM, A("ft", lo, hi)), (N16, A("zt", lo, hi))]))
+        affine(A("kt", lo, hi), bank, 1.0, 3072.0)
+    ms(A("zt", 0, TB), 192.0)
+    ts(A("ft", 0, TB), io, 0.0, ALU.mult, E(2), ALU.add)
+    ts(A("fc", 0, 256), A("nkc"), 1.0 / 128, ALU.mult, 191.50390625, ALU.add)
+    ts(A("nki", 0, 256), A("nkc"), 2, ALU.arith_shift_right, 31, ALU.bitwise_and)
+    cp(A("fc", 256, 512), A("nki", 0, 256))
+    ts(A("nki", 256, 512), A("nkc"), 3, ALU.bitwise_and)
+    for k in range(1, 4):
+        ts(A("fc", 256 + 256 * k, 512 + 256 * k), A("nki", 256, 512), float(k), ALU.is_equal)
+    for r in range(5):
+        dma("y", A("ft", TB, TB + W, 1, r, 128, 16), A("fc", 256 * r, 256 * r + 256), 65536 * (r + 1))
+    asel(A("st4"), A("zero"), [[-256, 9], [1, 16]], ALU.not_equal, 1.0, -79, 16)
+    asel(A("st15"), A("zero"), [[-256, 9], [1, 16]], ALU.not_equal, 1.0, -255, 16)
+    ts(PH, PC, 0.5, ALU.add)
+    ts(A("kb", 0, 6), A("io16", 0, 6), 16.0, ALU.mult, PH, ALU.add)
+    for t in range(4):
+        affine(A("lt4", 16 * t, 16 * t + 16), io, 16.0, PC)
+    iota(A("dmy"), [[0, 4], [16, 4]], TB + W, 0)
+    ts(A("dmy"), A("dmy"), PC, ALU.add)
+    iota(A("junk2"), [[1, 16], [0, 16]], 0, 0)
+    ts(A("tri"), A("junk2"), PC, ALU.is_gt)
+    ts(A("yw", 0, 8), A("gm"), YL, ALU.mult)
+    ts(A("yw", 8, 16), A("gm"), YG, ALU.mult)
+    ms(A("ob", 32, 48), 0.0)
+    ms(A("bw0", 1792, 2048), 16.0)
+
+    nchunk = [0]
+
+    def step(t, s, b):
+        bw = "bw%d" % t
+        c0, c1 = LB * b, LB * b + LB
+        pin = A(bw, c0, c1) if s % 2 == 0 else A("pb", c0, c1)
+        pout = A("pb", c0, c1) if s % 2 == 0 else A(bw, c0, c1)
+        dd, stile = A(bw, 256 + c0, 256 + c1), A(bw, 768 + c0, 768 + c1)
+        hsb = "hs0" if (t, s) == (0, 0) else "hs"
+
+        def L(name):
+            return A(name, c0, c1)
+
+        def R(k, bank="ps%d" % (2 + b)):
+            return A(bank, k * LB, (k + 1) * LB)
+        pe((R(0), [(WU, pin)]), (R(1), [(WV, pin)]), (R(2), [(LCM, stile)]))
+        cp(L("usb"), R(0))
+        tt(L("tt"), L("usb"), R(1), ALU.mult)
+        tt(L("xi"), L("tt"), R(2), ALU.add)
+        ts(L("hi"), L("xi"), 5, ALU.arith_shift_right, W - 1, ALU.bitwise_and)
+        cp(L("off"), L("hi"))
+        ts(L(hsb), L("off"), -2048.0, ALU.add)
+        n = nchunk[0]
+        nchunk[0] += 1
+        kg, nq = "kg%d" % (n % NKG), "nq%d" % (n % NNQ)
+        vg = CFG["vg"].get((s, b), 0)
+        copy("s", A(kg, 0, 16 * (LB - vg)), IND(A("kt", TB, TB + W), A("off", c0, c1 - vg)))
+        if vg:
+            copy("v", A(kg, 16 * (LB - vg), 16 * LB), IND(A("kt", TB, TB + W), A("off", c1 - vg, c1)))
+
+        def key(m):
+            return A(kg, m - 1, 16 * LB, 16)
+
+        def block(mi, bank):
+            return (R(mi, bank), [(M(mi, "f3"), pin), (M(mi, "f1"), key(9 + mi)), (M(mi, "f2"), key(7 - mi))])
+        na, pc = CFG["na"], CFG["pc"]
+        pe((R(7, "ps0"), [(IDM, pin)]))
+        for mi in range(0, na, pc):
+            pe(*[block(j, "ps0") for j in range(mi, min(na, mi + pc))])
+        for mi in range(na, 7, pc):
+            pe(*[block(j, "ps1") for j in range(mi, min(7, mi + pc))])
+        ts(A(nq, LB, (na + 1) * LB), A("ps0", 0, na * LB), 0.0, ALU.not_equal)
+        tt(R(0, nq), key(8), R(7, "ps0"), ALU.not_equal)
+        tt(R(8, nq), key(16), R(7, "ps0"), ALU.not_equal)
+        ts(A(nq, (na + 1) * LB, 8 * LB), A("ps1", na * LB, 7 * LB), 0.0, ALU.not_equal)
+        pe((R(0), [(M(mi, "f4"), R(mi, nq)) for mi in list(range(1, na + 1)) + [0, 8]]), stop=False)
+        pe((R(0), [(M(mi, "f4"), R(mi, nq)) for mi in range(na + 1, 8)]), start=False)
+        ts(L("mat"), R(0), THR, ALU.is_le)
+        pe((R(1), [(IDM, L(hsb)), (PEN, L("mat"))]), (R(2), [(SFX, L("mat"))]))
+        ts(L("ohh"), R(1), -8192.0, ALU.add, -2050.0, ALU.max)
+        ts(L("mm"), R(2), 255.0, ALU.add, 192.0, ALU.max)
+        pe((R(3), [(IDM, A("dbig", LB, 2 * LB)), (BON, L("ohh"))]))
+        scan(L("sc"), A("dbig", 0, LB), R(3), 0.0, ALU.add, ALU.min)
+        o2 = A("off2", 16 * s + c0 // 16, 16 * s + c1 // 16)
+        ts(o2, A("sc", c0 + 15, c1, 16), 32814.0, ALU.add)
+        fg = A("fg", 256 * s + c0, 256 * s + c1)
+        copy(en(("fg", s)), fg, IND(A("ft", 0, TB + W), o2))
+        tt(L("tz"), IND(A("zt", 0, TB + W), o2), L("mm"), ALU.subtract)
+        pe((R(0), [(K1R, fg)]), (R(2), [(SM, stile), (FM, fg)]))
+        if s == ST - 1:
+            pe((R(4), [(K3R, A("fg", 256 * j + c0, 256 * j + c1)) for j in range(ST)]))
+            act(L("ncb"), R(4), ACT.Relu, 1.0, -1.0)
+            scan(A("ncb", 256 + c0, 256 + c1), L("ncb"), L("ncb"), C("ncb", 255 + c0) if b else 0.0, ALU.add, ALU.max)
+        tt(L("eb"), R(0), dd, ALU.mult)
+        ts(stile, R(2), SBI, ALU.add, 0.0, ALU.max)
+        pe((R(1), [(IDM, pin), (SFX, L("mat")), (IDM, L("eb")), (Q16, stile)]))
+        tt(pout, R(1), L("tz"), ALU.max)
+        pd = R(0, "ps%d" % (6 + b % 2))
+        pe((pd, [(IDM, pin), (IDM, dd), (DM, stile), (NID, pout)]))
+        act(dd, pd, ACT.Relu)
+        if (t, s) == (RO - 1, ST - 1):
+            pe((R(5), [(IDM, pout), (X16, stile), (IDM, dd)]))
+            affine(A(bw, 1792 + c0, 1792 + c1), R(5), 1.0, -16.0)
+
+    def finish(t):
+        bw, snd = "bw%d" % t, "snd%d" % t
+        last = t == RO - 1
+        tiles = [0, 1, 3] if last else [0, 1, 2, 3]
+        nt = len(tiles)
+        own = [0, 1792 if last else 256, 512, 768]
+        valued = [1024, 1024 if last else 1792, 1024, 1280]
+        spare = [512, 512 if last else 1792, 512, 1536]
+        ts(A("cout%d" % t), A("ncb", 504, 512), float(CAP), ALU.min, 4096.0, ALU.mult)
+        send(t, 2 * t, A("cout%d" % t), A("cin%d" % t), 2500.0 if last else 4500.0)
+        for c in range(6):
+            act(A("junk", 0, 192), A("ncb", 256, 448), ACT.Sign, C("kb", c), -1.0, C("cn", c))
+        ts(A("cn", 0, 4), A("cn", 0, 4), 256.0, ALU.add)
+        ts(A("cn", 4, 6), A("cn", 4, 6), 192.0, ALU.add)
+        for c in range(4):
+            act(A("junk", 192, 256), A("ncb", 448, 512), ACT.Sign, C("kb", c), -1.0, C("cn", 8 + c))
+        for c in range(4, 6):
+            j2 = A("junk2", 64 * (c - 4), 64 * (c - 3))
+            ts(j2, A("ncb", 448, 512), C("kb", c), ALU.is_le, 2.0, ALU.mult)
+            add("v", "red", (C("cn", 8 + c), j2), [C("cn", 8 + c)], [j2], 64.0)
+        tt(A("cn", 16, 22), A("cn", 0, 6), A("cn", 8, 14), ALU.add)
+        ts(A("lst", 0, 6), A("cn", 16, 22), 0.5, ALU.mult, 255.0, ALU.min)
+        for n, tl in enumerate(tiles):
+            copy(en(("snd", t, tl), "s" if tl in (1, 2) else "v"), A(snd, CAP * n, CAP * n + CAP), IND(A(bw, own[tl], own[tl] + 256), A("lst", 0, 6)))
+        send(t, 2 * t + 1, A(snd, 0, CAP * nt), A(bw, ARR, ARR + CAP * nt), 3000.0 if last else 5000.0)
+        to_t(A("ps0", 0, 64), "st4", "fg", 0, 1024)
+        for s in range(ST):
+            ts(A("atw", 16 * s, 16 * s + 16), A("off2", 16 * s, 16 * s + 16), 8192.0 * (ST - s), ALU.add)
+        tt(A("cod"), A("ps0", 0, 64), A("atw"), ALU.mult)
+        tt(A("cod2"), A("cod", 0, 32), A("cod", 32, 64), ALU.max)
+        tt(A("codi", 0, 16), A("cod2", 0, 16), A("cod2", 16, 32), ALU.max)
+        ts(A("codi", 16, 32), A("codi", 0, 16), 8191, ALU.bitwise_and)
+        cp(A("atv"), A("codi", 16, 32))
+        affine(A("zz"), IND(A("zt", 0, TB + W), A("atv")), 1.0, -192.0)
+        act(A("fv"), IND(A("ft", 0, TB + W), A("atv")), ACT.Copy)
+        pe((A("ps3", 0, 256), [(IDM, A(bw, 512, 768)), (IDM, A("zz"))]))
+        ts(A("tb"), A("ps3", 0, 256), 16.0, ALU.is_ge, -16.0, ALU.mult)
+        if last:
+            tt(A(bw, 1024, 1280), A("ps3", 0, 256), A("tb"), ALU.add)
+        else:
+            pe((A("ps3", 256, 512), [(IDM, A(bw, 512, 768)), (IDM, A("zz")), (IDM, A("tb"))]))
+            act(A(bw, 1024, 1280), A("ps3", 256, 512), ACT.Copy)
+        pe((A("ps4", 0, 256), [(VM, A("fv"))]), (A("ps4", 256, 512), [(FFM, A(bw, 768, 1024))]))
+        affine(A(bw, 1280, 1536), A("ps4", 0, 256), 1.0, VBI)
+        act(A(bw, 1536, 1792), A("ps4", 256, 512), ACT.Copy)
+        to_t(A("ps2", 0, 32), "st4", "ncb", 0, 512)
+        act(A("nct"), A("ps2", 0, 32), ACT.Copy)
+        nd, cu = A("nct", 0, 16), A("nct", 16, 32)
+        if not last:
+            affine(A("zraw"), A("zz"), 1.0, 192.0)
+            ts(A("so1"), nd, 10000.0, ALU.mult)
+            tt(A("pls"), A("plt"), A("so1"), ALU.add)
+
+            def eq(c):
+                return A("eqb", c, 16 * (63 - 16 * (c % 4)) + c + 1, 16)
+            for c in range(16):
+                ts(eq(c), A("prow", 16 * c, 64 * (c // 4) + 64), C("pls", c), ALU.is_equal)
+                ops[-1]["wr"] = [("eqc", c, c + 1)]
+            tt(A("eqb", 0, 256), A("eqb", 0, 256), A("tri"), ALU.mult)
+            ops[-1]["rd"] = ops[-1]["rd"] + [("eqc", 0, 16)]
+            pe(*[(A("ps6", 64 * k, 64 * k + 64), [(IDM, A("ncb", 64 * k, 64 * k + 64))]
+                  + [(A("ps6", 16 * c, 64 * k + 64), BON, eq(c)) for c in range(4 * k + 3, 4 * k - 1, -1)]) for k in range(4)])
+            ts(A("win"), A("ps6", 0, 256), 0.0, ALU.is_equal)
+            to_t(A("ps7", 0, 16), "st4", "win", 0, 256)
+            tt(A("so1"), A("ps7", 0, 16), A("pld"), ALU.mult)
+            tt(A("so2"), A("so1"), A("dmy"), ALU.add)
+            cp(A("sof"), A("so2"))
+            for nm, src, lo in (("kt", bw, 512), ("ft", "fv", 0), ("zt", "zraw", 0)):
+                for k in range(3, -1, -1):
+                    cp(IND(A(nm), A("sof", 4 * k, 4 * k + 4)), A(src, lo + 64 * k, lo + 64 * k + 64))
+        ts(A("lv"), cu, CAP + 0.5, ALU.is_le)
+        tt(A("lv"), A("lv"), nd, ALU.mult)
+        ts(A("cux", 0, 16), nd, -1000.0, ALU.mult, 1000.0, ALU.add)
+        tt(A("cux", 16, 32), A("cux", 0, 16), cu, ALU.add)
+        cux = A("cux", 16, 32)
+        for n, tl in enumerate(tiles):
+            sl = (16 * n, 16 * n + 16)
+            affine(A("oa", *sl), nd, float(own[tl] - valued[tl]), float(valued[tl]))
+            if spare[tl] != own[tl]:
+                affine(A("ob", *sl), A("lv"), float(spare[tl] - own[tl]))
+            affine(A("ca", *sl), cux, 1.0, ARR + CAP * n - 1.0)
+            affine(A("cx", *sl), cux, -4095.0, ARR + CAP * n - 1.0)
+        wd = (0, 16 * nt)
+        tt(A("oa", *wd), A("oa", *wd), A("lt4", *wd), ALU.add)
+        tt(A("o0", *wd), A("oa", *wd), A("ob", *wd), ALU.add)
+        ts(A("aa", *wd), A("cx", *wd), C("cin%d" % t, 7), ALU.add)
+        tt(A("aa", *wd), A("aa", *wd), A("ca", *wd), ALU.min)
+        tt(A("ab", *wd), A("aa", *wd), A("o0", *wd), ALU.max)
+        cp(A("aof", *wd), A("ab", *wd))
+        win = A(bw, 0, ARR + CAP * nt)
+        if not last:
+            for lo, hi in ((0, 8), (48, 56), (8, 16), (56, 64), (16, 32), (32, 48)):
+                copy(en(("asm", lo), "s"), A("bw1", 16 * lo, 16 * hi), IND(win, A("aof", lo, hi)))
+        else:
+            for lo, hi, eng in ((32, 40, "v"), (40, 48, "s"), (0, 16, "v"), (16, 32, "s")):
+                copy(eng, A("outb", 16 * lo, 16 * hi), IND(win, A("aof", lo, hi)))
+            dma("y", ("ext", "yp", full), A("outb", 0, 512), 131072)
+            pe((A8("ps0", 0, 256), [(A("yw", 0, 8), A("outb", 512, 768))]))
+            pe((A8("ps1", 0, 256), [(A("yw", 8, 16), A("outb", 512, 768))]))
+            act(A8("yno", 0, 256), A8("ps0", 0, 256), ACT.Copy)
+            cp(A8("yno", 256, 512), A8("ps1", 0, 256))
+            dma("s", ("ext", "yn", full), A8("yno", 0, 512), 16384)
+
+    for t in range(RO):
+        for s in range(ST):
+            for b in range(NB):
+                step(t, s, b)
+            if (t, s) == (0, 1):
+                pe((A("ps6", 256, 512), [(R15, A("hs0"))]))
+                cp(A("prow"), A("ps6", 256, 512))
+                to_t(A("ps7", 256, 272), "st15", "hs0", 0, 256)
+                cp(A("plt"), A("ps7", 256, 272))
+                ts(A("so2"), A("plt"), 2048.0 + TB, ALU.add)
+                tt(A("pld"), A("so2"), A("dmy"), ALU.subtract)
+        finish(t)
+    return ops
+
+
+def depend(ops):
+    hist, banks = {}, {}
+    for n, op in enumerate(ops):
+        deps = set()
+        for name, lo, hi in op["rd"]:
+            for m, a, b, w in hist.get(name, []):
+                if w and a < hi and lo < b:
+                    deps.add(m)
+        for name, lo, hi in op["wr"]:
+            for m, a, b, w in hist.get(name, []):
+                if a < hi and lo < b and not (op["kind"] == "dma" and ops[m]["kind"] == "dma"):
+                    deps.add(m)
+        for name in set(r[0] for r in op["rd"] + op["wr"] if r[0].startswith("ps")):
+            cur, prev, eng = banks.get(name, ([], [], None))
+            if eng == op["eng"]:
+                deps.update(prev)
+                banks[name] = (cur + [n], prev, eng)
+            else:
+                deps.update(cur)
+                banks[name] = ([n], cur, op["eng"])
+        if op["kind"] == "arrive":
+            deps = {op["args"][1]}
+        for name, lo, hi in op["wr"]:
+            if op["kind"] != "dma":
+                hist[name] = [h for h in hist.get(name, []) if not (lo <= h[1] and h[2] <= hi and h[0] in deps)]
+            hist.setdefault(name, []).append((n, lo, hi, True))
+        for name, lo, hi in op["rd"]:
+            hist.setdefault(name, []).append((n, lo, hi, False))
+        deps.discard(n)
+        op["deps"] = sorted(deps)
+
+
+def schedule(ops):
+    n = len(ops)
+    users = [[] for _ in range(n)]
+    for k, op in enumerate(ops):
+        for d in op["deps"]:
+            users[d].append(k)
+    rest = [0.0] * n
+    nxt = 0.0
+    for k in range(n - 1, -1, -1):
+        rest[k] = ops[k]["cost"] + ops[k]["lat"] + max([CFG["hop"] + rest[u] for u in users[k]] + [0.0])
+        if ops[k]["eng"] == "s" and any(w[0].startswith("kg") for w in ops[k]["wr"]):
+            rest[k] = nxt = max(rest[k], nxt + CFG["pace"] * ops[k]["cost"])
+    x = CFG["seed"]
+    for k in range(n):
+        x = (x * 1103515245 + 12345) % 2147483648
+        rest[k] += CFG["noise"] * x / 2147483648
+    left = [len(op["deps"]) for op in ops]
+    ready = {k: 0.0 for k in range(n) if left[k] == 0}
+    free, order, end = {}, [], [0.0] * n
+    while ready:
+        start = {k: max(r, free.get(ops[k]["eng"], 0.0)) for k, r in ready.items()}
+        first = min(start, key=lambda k: (start[k], -rest[k]))
+        eng = ops[first]["eng"]
+        k = max((j for j in start if ops[j]["eng"] == eng and start[j] <= start[first] + CFG["slack"]), key=lambda j: (rest[j], -j))
+        del ready[k]
+        free[eng] = start[k] + ops[k]["cost"]
+        end[k] = free[eng] + ops[k]["lat"]
+        ops[k]["start"] = start[k]
+        order.append(k)
+        for u in users[k]:
+            left[u] -= 1
+            if left[u] == 0:
+                ready[u] = max(end[d] + (CFG["self"] if ops[d]["eng"] == ops[u]["eng"] else CFG["hop"]) for d in ops[u]["deps"])
+    return order, max(end)
+
+
+def plan():
+    ops = build_ops()
+    depend(ops)
+    order, total = schedule(ops)
+    count, clock = {}, {}
+    for k in order:
+        op = ops[k]
+        eng, kind = op["eng"], op["kind"]
+        ck = clock.setdefault(eng, {})
+        waits = {}
+        if kind != "arrive":
+            for d in sorted(op["deps"], key=lambda j: -ops[j]["start"]):
+                sem, val = ops[d]["tok"]
+                if ck.get(sem, 0) < val:
+                    waits[sem] = max(waits.get(sem, 0), val)
+                    for s2, v2 in ops[d]["clock"].items():
+                        ck[s2] = max(ck.get(s2, 0), v2)
+        op["waits"] = sorted(waits.items())
+        if kind == "dma":
+            tok = ("d%d" % op["args"][2], 16)
+        elif kind == "arrive":
+            tok = ("ar%d" % op["args"][0], 1)
+        elif kind == "send":
+            tok = ("ls", 1)
+        else:
+            sem = "s" + eng
+            count[sem] = count.get(sem, 0) + (len(op["args"]) if kind == "mm" else 1)
+            tok = (sem, count[sem])
+        op["tok"] = tok
+        op["clock"] = {} if kind == "arrive" else dict(ck)
+        op["clock"][tok[0]] = tok[1]
+    return ops, order, total, count
+
+
+PLAN = []
+
+
+def route(T, topo, t, r):
+    n = len(T.cores)
+    src, dst = T.cores[r], T.cores[(r + 1 + t) % n]
+    if topo.may_write(src, dst):
+        return dst, None, topo.mask(src, dst)
+    able = [c for c in topo.cores_of(src) if c != src and topo.may_write(c, dst)]
+    able.sort(key=lambda c: (topo.die(c) != topo.die(src), c))
+    return dst, able[0], topo.mask(src, able[0]) & topo.mask(able[0], dst)
+
+
+def engines_in(mask):
+    return bin(mask).count("1")
+
+
+def rank_program(g, core, T, topo):
+    if not PLAN:
+        PLAN.append(plan())
+    ops, order, total, count = PLAN[0]
+    n = len(T.cores)
+    rank = T.rank_of(core)
+    sent = 0
+    if rank is None:
+        for k in order:
+            if ops[k]["kind"] == "send":
+                t, m, src, land = ops[k]["args"]
+                for r in range(n):
+                    dst, via, mask = route(T, topo, t, r)
+                    if via == core:
+                        g.wait_ge(T.sem["ar%d" % m], engines_in(mask))
+                        rid, pid = topo.addr(dst, core)
+                        g.remote_dma(real(T, land), real(T, land), T.sem["ar%d" % m], T.sem.hl, pid, rid, mask)
+                        sent += engines_in(mask)
+        if sent:
+            g.wait_ge(T.sem.hl, sent)
+        return
+    arrive = [engines_in(route(T, topo, t, (rank - 1 - t) % n)[2]) for t in range(RO)]
+    queue = {"v": g.vector, "s": g.scalar, "p": g.tensor, "g": g, "y": g.sync}
+    for k in order:
+        op = ops[k]
+        kind, a = op["kind"], op["args"]
+        if kind == "arrive":
+            continue
+        q = queue[op["eng"]]
+        for sem, val in op["waits"]:
+            q.wait_ge(T.sem[sem], arrive[int(sem[2]) // 2] if sem.startswith("ar") else val)
+        sem = T.sem[op["tok"][0]]
+        if kind == "mm":
+            for terms in a:
+                for j, (o, l, rr) in enumerate(terms):
+                    ins = q.matmul(real(T, o), real(T, l), real(T, rr), j == 0 and op["ends"][0], j == len(terms) - 1 and op["ends"][1])
+                ins.then_inc(sem, 1)
+            continue
+        r = [real(T, x) for x in a]
+        if kind == "send":
+            dst, via, mask = route(T, topo, a[0], rank)
+            rid, pid = topo.addr(dst if via is None else via, core)
+            g.remote_dma(r[3], r[2], T.sem["ar%d" % a[1]], sem, pid, rid, mask)
+            sent += engines_in(mask)
+        elif kind == "dma":
+            q.dma_start(r[0], r[1]).then_inc(sem, 16)
+        elif kind == "ts":
+            if a[5] is None:
+                q.tensor_scalar(r[0], r[1], r[2], None, r[4]).then_inc(sem, 1)
+            else:
+                q.tensor_scalar(r[0], r[1], r[2], r[3], r[4], r[5]).then_inc(sem, 1)
+        elif kind == "tt":
+            q.tensor_tensor(r[0], r[1], r[2], r[3]).then_inc(sem, 1)
+        elif kind == "cp":
+            q.tensor_copy(r[0], r[1]).then_inc(sem, 1)
+        elif kind == "ms":
+            q.memset(r[0], r[1]).then_inc(sem, 1)
+        elif kind == "scan":
+            q.tensor_tensor_scan(r[0], r[1], r[2], r[3], r[4], r[5]).then_inc(sem, 1)
+        elif kind == "red":
+            q.tensor_reduce(r[0], r[1], AxisListType.X, ALU.add).then_inc(sem, 1)
+        elif kind == "act":
+            q.activation(r[0], r[1], r[2], bias=r[3], scale=r[4], accum_out=r[5]).then_inc(sem, 1)
+        elif kind == "iota":
+            if SB[a[0][1]][1] == I32:
+                q.iota(r[0], r[1], r[2], r[3]).then_inc(sem, 1)
+            else:
+                q.iota(r[0], r[1], r[2], r[3], allow_small_or_imprecise_dtypes=True).then_inc(sem, 1)
+        elif kind == "asel":
+            q.affine_select(r[0], r[1], r[2], r[3], r[4], r[5], r[6]).then_inc(sem, 1)
+    for op in ops:
+        if op["kind"] == "dma":
+            g.sync.wait_ge(T.sem[op["tok"][0]], 16)
+    for sem, val in sorted(count.items()):
+        g.sync.wait_ge(T.sem[sem], val)
+    g.wait_ge(T.sem.ls, sent)

@@ -10,11 +10,10 @@ NB = Q // LB
 NKG, NNQ = 3, 2
 ARR, AW = 2048, 384
 BF, F32, I32, U16, F16 = "bfloat16", "float32", "int32", "uint16", "float16"
-CFG = {"gcyc": 1.5, "pe": 0.5, "hop": 100.0, "self": 60.0, "pace": 1.1, "slack": 40.0, "seed": 16, "noise": 100.0,
-       "vg": {(0, 0): 32}, "na": 3, "pc": 2,
-       "e": {("snd", 1, 0): "s", ("snd", 0, 3): "s", ("snd", 1, 1): "v", ("asm", 0): "v", ("asm", 32): "v",
-             ("fg", 0): "s", ("fg", 3): "s"}}
-
+CFG = {"gcyc": 1.7, "pe": 0.9, "hop": 200.0, "self": 200.0, "pace": 1.3, "slack": 120.0, "cyc": 0.9, "fix": 20.0,
+       "sfix": 100.0, "vg": {(0, 0): 32}, "nd": 2, "na": 3, "pc": 2,
+       "e": {("snd", 0, 3): "s", ("snd", 0, 2): "v", ("snd", 1, 1): "v", ("snd", 1, 3): "s", ("asm", 48): "v",
+             ("d16", 3): "s", "oa": "v", "ob": "v", "ca": "v", "cx": "v"}}
 SB = {
     "ft": (TW, BF), "zt": (TW, BF), "kt": (TW, BF),
     "bw0": (ARR + AW, BF), "bw1": (ARR + AW, BF), "outb": (768, BF), "pb": (256, BF),
@@ -22,8 +21,8 @@ SB = {
     "wti": (2, I32), "wtf": (2, F32), "nkc": (256, I32), "nki": (512, I32), "fc": (1280, BF),
     "qni": (256, I32), "qnh": (256, BF), "qnf": (256, F16), "g8": (256, BF), "ones": (128, BF), "zero": (144, BF),
     "iop": (4, I32), "col": (32, F32), "io16": (16, F32), "xio": (128, BF), "ee": (16, F32), "rm": (16, F32), "gm": (8, F32),
-    "mx": (128 * 18, BF), "st4": (144, BF), "st15": (144, BF), "tg": (32, F32), "pt5": (64, BF),
-    "f1": (896, BF), "f2": (896, BF), "f3": (896, BF), "f4": (1152, BF), "f5": (512, BF),
+    "mx": (128 * 19, BF), "st4": (144, BF), "st15": (144, BF), "tg": (32, F32), "pt5": (64, BF),
+    "f1": (896, BF), "f2": (896, BF), "f3": (896, BF), "f4": (1152, BF), "f6": (1024, BF), "f5": (512, BF),
     "yw": (16, BF), "kb": (8, F32), "lt4": (64, F32), "dmy": (16, F32), "tri": (256, BF), "dbig": (128, BF),
     "usb": (256, F32), "tt": (256, F32), "xi": (256, I32), "hi": (256, I32), "off": (256, U16),
     "hs": (256, F16), "hs0": (256, F16), "mat": (256, BF), "ohh": (256, F16), "mm": (256, BF), "sc": (256, F32),
@@ -39,7 +38,7 @@ SB = {
 for _k in range(NKG):
     SB["kg%d" % _k] = (16 * LB, BF)
 for _k in range(NNQ):
-    SB["nq%d" % _k] = (9 * LB, BF)
+    SB["nq%d" % _k] = (13 * LB, BF)
 SCRATCH = {k: ("sbuf", [128, v[0]], v[1]) for k, v in SB.items()}
 for _k in range(8):
     SCRATCH["ps%d" % _k] = ("psum", [128, 512], F32)
@@ -113,7 +112,8 @@ def build_ops():
                 wr += regions(o)
         for i in ins:
             rd += regions(i)
-        ops.append({"eng": eng, "kind": kind, "args": args, "wr": wr, "rd": rd, "cost": cost, "lat": lat})
+        ops.append({"eng": eng, "kind": kind, "args": args, "wr": wr, "rd": rd, "lat": lat,
+                    "cost": cost * CFG["cyc"] + (CFG["fix"] if eng in "vs" else 0) + (CFG["sfix"] if eng == "s" else 0)})
 
     def vcost(out, ins, tt=False):
         if out[0] == "ind":
@@ -152,11 +152,14 @@ def build_ops():
         else:
             act(out, in0, ACT.Copy)
 
-    def affine(out, in0, scale, bias=0.0):
-        act(out, in0, ACT.Identity, bias, scale)
-
     def en(name, dflt="v"):
         return CFG["e"].get(name, dflt)
+
+    def affine(out, in0, scale, bias=0.0):
+        if en(out[1], "s") == "v":
+            ts(out, in0, scale, ALU.mult, bias, ALU.add)
+        else:
+            act(out, in0, ACT.Identity, bias, scale)
 
     def pe(*groups, start=True, stop=True):
         outs, ins, cost, gs = [], [], 0.0, []
@@ -217,7 +220,6 @@ def build_ops():
     dma("s", A8("qni", 0, 256), ("ext", "qn", full), 8192)
     dma("s", A("wti"), ("ext", "wt", full), 1024)
     dma("y", A("nkc"), ("ext", "nk", full), 1200000)
-
     ms(A("ones"), 1.0)
     iota(A("iop", 0, 1), [[0, 1]], 0, 1)
     iota(io, [[1, 16]], 0, 0)
@@ -279,6 +281,11 @@ def build_ops():
     tt(A("tg", 0, 9), A("tg", 0, 9), A("tg", 16, 25), ALU.add)
     for mi in range(9):
         ts(M(mi, "f4"), A("xio"), C("tg", mi), ALU.is_equal, C("rm", 7 if mi == 0 else 15), ALU.mult)
+    nd_ = CFG["nd"]
+    direct = [m for j in range(nd_) for m in (9 + j, 7 - j)]
+    ts(A("tg", 16, 32), io, G7, ALU.add, -7.0, ALU.add)
+    for j, m in enumerate(direct):
+        ts(M(j, "f6"), A("xio"), C("tg", 15 + m), ALU.is_equal, C("rm", m - 1), ALU.mult)
     ts(THR, PC, 0.25, ALU.mult, 0.25, ALU.add)
     affine(SFX, LT, -63.0)
     affine(PEN, LT, -8192.0)
@@ -297,15 +304,15 @@ def build_ops():
     tt(P5(0, 0, 2), E(4, 2), E(6, 2), ALU.add)
     tt(P5(0, 4, 6), E(4, 2), E(6, 2), ALU.add)
     cp(P5(0, 8, 10), E(8, 2))
-    ts(P5(0, 11, 12), E(12), -1.0, ALU.mult)
     cp(P5(0, 13, 14), E(12))
+    ts(P5(0, 11, 12), E(12), -1.0, ALU.mult)
+    cp(P5(1, 11, 12), E(2))
     ts(A("col", C32, C32 + 2), E(2, 2), 32.0, ALU.mult)
     ts(A("col", CM32, CM32 + 2), E(2, 2), -32.0, ALU.mult)
     ts(P5(1, 0, 2), E(0, 2), 0.0, ALU.mult, C("col", C32), ALU.add)
     ts(P5(1, 2, 4), E(0, 2), C("col", CM32), ALU.add)
     ts(P5(1, 4, 6), E(0, 2), 0.0, ALU.mult, C("col", CM32 + 1), ALU.add)
     ts(P5(1, 6, 8), E(0, 2), C("col", C32 + 1), ALU.add)
-    cp(P5(1, 11, 12), E(2))
     tt(P5(1, 12, 13), E(2), E(3), ALU.add)
     for j in (0, 4, 8):
         cp(P5(2, j, j + 2), E(0, 2))
@@ -317,7 +324,6 @@ def build_ops():
         dst = SBI if n == 4 else C("col", 26 + n)
         ts(dst, E(r), wv, ALU.mult, prev, ALU.add)
         prev = dst
-
     for k in range(8):
         lo, hi = TB + 512 * k, TB + 512 * k + 512
         bank = A("ps%d" % (0, 1, 3, 6, 7)[k % 5])
@@ -348,7 +354,6 @@ def build_ops():
     ts(A("yw", 8, 16), A("gm"), YG, ALU.mult)
     ms(A("ob", 32, 48), 0.0)
     ms(A("bw0", 1792, 2048), 16.0)
-
     nchunk = [0]
 
     def step(t, s, b):
@@ -386,15 +391,21 @@ def build_ops():
             return (R(mi, bank), [(M(mi, "f3"), pin), (M(mi, "f1"), key(9 + mi)), (M(mi, "f2"), key(7 - mi))])
         na, pc = CFG["na"], CFG["pc"]
         pe((R(7, "ps0"), [(IDM, pin)]))
-        for mi in range(0, na, pc):
+        for mi in range(nd_, na, pc):
             pe(*[block(j, "ps0") for j in range(mi, min(na, mi + pc))])
         for mi in range(na, 7, pc):
             pe(*[block(j, "ps1") for j in range(mi, min(7, mi + pc))])
-        ts(A(nq, LB, (na + 1) * LB), A("ps0", 0, na * LB), 0.0, ALU.not_equal)
+
+        def slot(j):
+            return R(1 + j if j < nd_ else 9 + j - nd_, nq)
+        for j, m in enumerate(direct):
+            tt(slot(j), key(m), R(7, "ps0"), ALU.not_equal)
+        ts(A(nq, (nd_ + 1) * LB, (na + 1) * LB), A("ps0", nd_ * LB, na * LB), 0.0, ALU.not_equal)
         tt(R(0, nq), key(8), R(7, "ps0"), ALU.not_equal)
         tt(R(8, nq), key(16), R(7, "ps0"), ALU.not_equal)
         ts(A(nq, (na + 1) * LB, 8 * LB), A("ps1", na * LB, 7 * LB), 0.0, ALU.not_equal)
-        pe((R(0), [(M(mi, "f4"), R(mi, nq)) for mi in list(range(1, na + 1)) + [0, 8]]), stop=False)
+        pe((R(0), [(M(mi, "f4"), R(mi, nq)) for mi in list(range(nd_ + 1, na + 1)) + [0, 8]]
+            + [(M(j, "f6"), slot(j)) for j in range(2 * nd_)]), stop=False)
         pe((R(0), [(M(mi, "f4"), R(mi, nq)) for mi in range(na + 1, 8)]), start=False)
         ts(L("mat"), R(0), THR, ALU.is_le)
         pe((R(1), [(IDM, L(hsb)), (PEN, L("mat"))]), (R(2), [(SFX, L("mat"))]))
@@ -405,7 +416,7 @@ def build_ops():
         o2 = A("off2", 16 * s + c0 // 16, 16 * s + c1 // 16)
         ts(o2, A("sc", c0 + 15, c1, 16), 32814.0, ALU.add)
         fg = A("fg", 256 * s + c0, 256 * s + c1)
-        copy(en(("fg", s)), fg, IND(A("ft", 0, TB + W), o2))
+        cp(fg, IND(A("ft", 0, TB + W), o2))
         tt(L("tz"), IND(A("zt", 0, TB + W), o2), L("mm"), ALU.subtract)
         pe((R(0), [(K1R, fg)]), (R(2), [(SM, stile), (FM, fg)]))
         if s == ST - 1:
@@ -418,7 +429,10 @@ def build_ops():
         tt(pout, R(1), L("tz"), ALU.max)
         pd = R(0, "ps%d" % (6 + b % 2))
         pe((pd, [(IDM, pin), (IDM, dd), (DM, stile), (NID, pout)]))
-        act(dd, pd, ACT.Relu)
+        if en(("d16", s)) == "s":
+            act(dd, pd, ACT.Relu)
+        else:
+            ts(dd, pd, 0.0, ALU.max)
         if (t, s) == (RO - 1, ST - 1):
             pe((R(5), [(IDM, pout), (X16, stile), (IDM, dd)]))
             affine(A(bw, 1792 + c0, 1792 + c1), R(5), 1.0, -16.0)
@@ -469,7 +483,7 @@ def build_ops():
         affine(A(bw, 1280, 1536), A("ps4", 0, 256), 1.0, VBI)
         act(A(bw, 1536, 1792), A("ps4", 256, 512), ACT.Copy)
         to_t(A("ps2", 0, 32), "st4", "ncb", 0, 512)
-        act(A("nct"), A("ps2", 0, 32), ACT.Copy)
+        cp(A("nct"), A("ps2", 0, 32))
         nd, cu = A("nct", 0, 16), A("nct", 16, 32)
         if not last:
             affine(A("zraw"), A("zz"), 1.0, 192.0)
@@ -585,10 +599,6 @@ def schedule(ops):
         rest[k] = ops[k]["cost"] + ops[k]["lat"] + max([CFG["hop"] + rest[u] for u in users[k]] + [0.0])
         if ops[k]["eng"] == "s" and any(w[0].startswith("kg") for w in ops[k]["wr"]):
             rest[k] = nxt = max(rest[k], nxt + CFG["pace"] * ops[k]["cost"])
-    x = CFG["seed"]
-    for k in range(n):
-        x = (x * 1103515245 + 12345) % 2147483648
-        rest[k] += CFG["noise"] * x / 2147483648
     left = [len(op["deps"]) for op in ops]
     ready = {k: 0.0 for k in range(n) if left[k] == 0}
     free, order, end = {}, [], [0.0] * n

from concourse.mybir import AluOpType, AxisListType, ActivationFunctionType

ALU = AluOpType
ACT = ActivationFunctionType
W, Q, CAP, ST, RO = 4096, 256, 96, 4, 2
TB = 16
TW = TB + W + 64
LB = 64
NB = Q // LB
NKG, NNQ = 3, 2
ARR, AW = 2048, 384
BF, F32, I32, U16, F16 = "bfloat16", "float32", "int32", "uint16", "float16"
CFG = {"gcyc": 1.7, "pe": 0.9, "hop": 200.0, "self": 200.0, "pace": 1.3, "slack": 120.0, "cyc": 0.9, "fix": 20.0,
       "sfix": 100.0, "vg": {(0, 0): 32}, "nd": 2, "na": 3, "pc": 2,
       "e": {("snd", 0, 3): "s", ("snd", 0, 2): "v", ("snd", 1, 1): "v", ("snd", 1, 3): "s", ("asm", 48): "v",
             ("d16", 3): "s", "oa": "v", "ob": "v", "ca": "v", "cx": "v"}}
SB = {
    "ft": (TW, BF), "zt": (TW, BF), "kt": (TW, BF),
    "bw0": (ARR + AW, BF), "bw1": (ARR + AW, BF), "outb": (768, BF), "pb": (256, BF),
    "snd0": (AW, BF), "snd1": (AW, BF), "cout0": (8, BF), "cout1": (8, BF), "cin0": (8, BF), "cin1": (8, BF),
    "wti": (2, I32), "wtf": (2, F32), "nkc": (256, I32), "nki": (512, I32), "fc": (1280, BF),
    "qni": (256, I32), "qnh": (256, BF), "qnf": (256, F16), "g8": (256, BF), "ones": (128, BF), "zero": (144, BF),
    "iop": (4, I32), "col": (32, F32), "io16": (16, F32), "xio": (128, BF), "ee": (16, F32), "rm": (16, F32), "gm": (8, F32),
    "mx": (128 * 19, BF), "st4": (144, BF), "st15": (144, BF), "tg": (32, F32), "pt5": (64, BF),
    "f1": (896, BF), "f2": (896, BF), "f3": (896, BF), "f4": (1152, BF), "f6": (1024, BF), "f5": (512, BF),
    "yw": (16, BF), "kb": (8, F32), "lt4": (64, F32), "dmy": (16, F32), "tri": (256, BF), "dbig": (128, BF),
    "usb": (256, F32), "tt": (256, F32), "xi": (256, I32), "hi": (256, I32), "off": (256, U16),
    "hs": (256, F16), "hs0": (256, F16), "mat": (256, BF), "ohh": (256, F16), "mm": (256, BF), "sc": (256, F32),
    "off2": (64, U16), "fg": (1024, BF), "tz": (256, BF), "eb": (256, BF),
    "ncb": (512, BF), "junk": (256, BF), "junk2": (256, BF), "cn": (24, F32), "lst": (8, U16),
    "atw": (64, F32), "cod": (64, F32), "cod2": (32, F32), "codi": (32, I32), "atv": (16, U16),
    "zz": (256, BF), "zraw": (256, BF), "fv": (256, BF), "tb": (256, BF),
    "prow": (256, F16), "plt": (16, F32), "pls": (16, F32), "pld": (16, F32), "eqb": (1024, BF), "win": (256, BF),
    "so1": (16, F32), "so2": (16, F32), "sof": (16, U16),
    "nct": (32, F32), "lv": (16, F32), "cux": (32, F32), "oa": (64, F32), "ob": (64, F32), "o0": (64, F32),
    "ca": (64, F32), "cx": (64, F32), "aa": (64, F32), "ab": (64, F32), "aof": (64, U16), "yno": (512, F32),
}
for _k in range(NKG):
    SB["kg%d" % _k] = (16 * LB, BF)
for _k in range(NNQ):
    SB["nq%d" % _k] = (13 * LB, BF)
SCRATCH = {k: ("sbuf", [128, v[0]], v[1]) for k, v in SB.items()}
for _k in range(8):
    SCRATCH["ps%d" % _k] = ("psum", [128, 512], F32)
SEMAPHORES = ["sv", "ss", "sp", "sg", "ls", "hl", "ar0", "ar1", "ar2", "ar3"] + ["d%d" % k for k in range(16)]
TWO = (BF, U16, F16)


def A(name, c0=0, c1=None, step=1, p0=0, p1=128, pstep=1):
    if c1 is None:
        c1 = 512 if name.startswith("ps") else SB[name][0]
    return ("ap", name, c0, c1, step, p0, p1, pstep)


def A8(name, c0, c1):
    return A(name, c0, c1, 1, 0, 8)


def C(name, c):
    return A(name, c, c + 1)


def IND(win, off):
    return ("ind", win, off)


def is_op(x):
    return isinstance(x, tuple)


def width(x):
    if x[0] == "ind":
        return 16 * width(x[2])
    return (x[3] - x[2] + x[4] - 1) // x[4]


def two_byte(x):
    return x[0] == "ap" and not x[1].startswith("ps") and SB[x[1]][1] in TWO


def regions(x):
    if not is_op(x) or x[0] == "ext":
        return []
    if x[0] == "ind":
        return regions(x[1]) + regions(x[2])
    return [(x[1], x[2], x[3])]


def real(T, x):
    if not is_op(x):
        return x
    if x[0] == "ind":
        return real(T, x[1]).indirect(real(T, x[2]))
    if x[0] == "ext":
        return T[x[1]][x[2]]
    rows = slice(x[5], x[6], x[7]) if x[7] != 1 else slice(x[5], x[6])
    cols = slice(x[2], x[3], x[4]) if x[4] != 1 else slice(x[2], x[3])
    return T[x[1]][rows, cols]


def build_ops():
    ops = []
    gc_ = CFG["gcyc"]

    def add(eng, kind, args, outs, ins, cost, lat=0.0):
        wr, rd = [], []
        for o in outs:
            if o[0] == "ind":
                wr += regions(o[1])
                rd += regions(o[2])
            else:
                wr += regions(o)
        for i in ins:
            rd += regions(i)
        ops.append({"eng": eng, "kind": kind, "args": args, "wr": wr, "rd": rd, "lat": lat,
                    "cost": cost * CFG["cyc"] + (CFG["fix"] if eng in "vs" else 0) + (CFG["sfix"] if eng == "s" else 0)})

    def vcost(out, ins, tt=False):
        if out[0] == "ind":
            return 50 + 3.5 * width(out)
        if ins and ins[0][0] == "ind":
            return 50 + gc_ * width(out)
        n = width(out)
        if tt:
            n = 2 * n if not any(i[1].startswith("ps") for i in ins) else n
        elif two_byte(out) and all(two_byte(i) for i in ins):
            n = n / 2
        return max(64.0, n)

    def ts(out, in0, s1, op0, s2=None, op1=None):
        add("v", "ts", (out, in0, s1, s2, op0, op1), [out], [in0, s1, s2], vcost(out, [in0]))

    def tt(out, in0, in1, op):
        add("v", "tt", (out, in0, in1, op), [out], [in0, in1], vcost(out, [in0, in1], True))

    def cp(out, in0):
        add("v", "cp", (out, in0), [out], [in0], vcost(out, [in0]))

    def ms(out, c):
        add("v", "ms", (out, c), [out], [], vcost(out, []))

    def scan(out, d0, d1, init, op0, op1):
        add("v", "scan", (out, d0, d1, init, op0, op1), [out], [d0, d1, init], float(width(out)))

    def act(out, in0, func, bias=0.0, scale=1.0, accum=None):
        n = 65 + gc_ * width(out) if in0[0] == "ind" else max(64.0, width(out)) + 20
        add("s", "act", (out, in0, func, bias, scale, accum), [out] + ([accum] if accum else []), [in0, bias, scale], n)

    def copy(eng, out, in0):
        if eng == "v":
            cp(out, in0)
        else:
            act(out, in0, ACT.Copy)

    def en(name, dflt="v"):
        return CFG["e"].get(name, dflt)

    def affine(out, in0, scale, bias=0.0):
        if en(out[1], "s") == "v":
            ts(out, in0, scale, ALU.mult, bias, ALU.add)
        else:
            act(out, in0, ACT.Identity, bias, scale)

    def pe(*groups, start=True, stop=True):
        outs, ins, cost, gs = [], [], 0.0, []
        for out, terms in groups:
            terms = [t if len(t) == 3 else (out, t[0], t[1]) for t in terms]
            gs.append(terms)
            for o, l, r in terms:
                outs.append(o)
                ins += [l, r]
                cost += CFG["pe"] * max(min(64, width(l)), width(r))
        add("p", "mm", gs, outs, ins, cost, 60.0)
        ops[-1]["ends"] = (start, stop)

    def iota(out, pattern, base, cm):
        add("g", "iota", (out, pattern, base, cm), [out], [], 150 + 2 * width(out))

    def asel(out, in0, pattern, op, fill, base, cm):
        add("g", "asel", (out, in0, pattern, op, fill, base, cm), [out], [in0], 190 + 2 * width(out))

    ndma = [0]

    def dma(q, out, in0, nbytes):
        add(q, "dma", (out, in0, ndma[0]), [out], [in0], 60.0, 1800 + nbytes / 200.0)
        ndma[0] += 1

    def send(t, n, src, dst, lat):
        add("g", "send", (t, n, src, dst), [], [src], 500.0)
        add("x", "arrive", (n, len(ops) - 1), [dst], [], 0.0, lat)

    def to_t(out, strip, src, lo, hi):
        pe((out, [(A(strip, 15 - i, 143 - i), A(src, lo + i, hi, 16)) for i in range(16)]))

    def M(k, name="mx"):
        return A(name, 128 * k, 128 * k + 128)

    IDM, NID, N16, JM, BON, UT, LT, WU, WV, PEN, SFX, LCM, K1R, K3R, Q16, DM, X16, R15 = [M(k) for k in range(18)]
    SM, FM, VM, FFM = [A("f5", k, 512, 4) for k in range(4)]

    def P5(m, j0, j1):
        return A("pt5", j0 * 4 + m, (j1 - 1) * 4 + m + 1, 4)

    (PC, GCOL, PF, QC, WP, YL, YG, LCW, THR, PH, SBI, VBI, T0, T1, T2, G7, P3, B0, T3) = [C("col", k) for k in range(19)]
    C32, CM32 = 22, 24

    def E(r, n=1):
        return A("ee", r, r + n)

    io, Z = A("io16"), A("zero", 0, 128)
    blk = [[-16, 8], [0, 16]]

    def row(out, in0, r, v):
        asel(out, in0, blk, ALU.not_equal, v, -r, 1)

    full = (slice(None), slice(None))
    for k in range(4):
        dma("y", A("ft", TB + 1024 * k, TB + 1024 * k + 1024), ("ext", "sen", (slice(None), slice(1024 * k, 1024 * k + 1024))), 262144 * (k + 1))
    dma("s", A("bw0", 0, 256), ("ext", "qp", full), 65536)
    dma("s", A8("qni", 0, 256), ("ext", "qn", full), 8192)
    dma("s", A("wti"), ("ext", "wt", full), 1024)
    dma("y", A("nkc"), ("ext", "nk", full), 1200000)
    ms(A("ones"), 1.0)
    iota(A("iop", 0, 1), [[0, 1]], 0, 1)
    iota(io, [[1, 16]], 0, 0)
    asel(IDM, A("ones"), [[1, 128]], ALU.is_equal, 0.0, 0, -1)
    ms(A("zero"), 0.0)
    affine(N16, IDM, -16.0)
    asel(NID, Z, [[1, 128]], ALU.not_equal, -1.0, 0, -1)
    asel(BON, A("ones"), blk, ALU.is_ge, 0.0, 0, 1)
    asel(BON, BON, [[16, 8], [0, 16]], ALU.is_ge, 0.0, 15, -1)
    asel(UT, BON, [[1, 128]], ALU.is_ge, 0.0, 0, -1)
    asel(A8("g8", 128, 256), A8("ones", 0, 128), [[4, 8], [0, 4], [1, 4]], ALU.is_equal, 0.0, -1, -4)
    asel(A8("g8", 0, 128), A8("ones", 0, 128), [[4, 8], [0, 4], [1, 4]], ALU.is_equal, 0.0, 0, -4)
    asel(A8("g8", 0, 128), A8("g8", 0, 128), [[4, 8], [0, 4], [1, 4]], ALU.not_equal, -32.0, -1, -4)
    asel(JM, A("ones"), [[-16, 8], [1, 16]], ALU.is_equal, 0.0, -15, 1)
    iota(A("xio"), [[1, 128]], 0, 0)
    asel(LT, BON, [[-1, 128]], ALU.is_ge, 0.0, 0, 1)
    cp(PF, A("iop", 0, 1))
    ts(A("iop", 1, 2), A("iop", 0, 1), 15, ALU.bitwise_and)
    cp(PC, A("iop", 1, 2))
    ts(GCOL, PF, PC, ALU.subtract, 0.0625, ALU.mult)
    ts(A("gm"), A("io16", 0, 8), GCOL, ALU.is_equal)
    ts(A("ee"), io, PC, ALU.is_equal)
    ts(A("rm"), io, PC, ALU.is_ge)
    ts(A("iop", 2, 3), A("iop", 0, 1), 2, ALU.arith_shift_right, 3, ALU.bitwise_and)
    ts(A("iop", 3, 4), A("iop", 0, 1), 3, ALU.bitwise_and)
    cp(QC, A("iop", 2, 3))
    cp(P3, A("iop", 3, 4))
    ts(T3, P3, 2.0, ALU.not_equal, P3, ALU.mult)
    ts(WP, T3, 0.0, ALU.is_equal, 31.0, ALU.mult)
    ts(WP, WP, 1.0, ALU.add)
    ts(YL, QC, 0.0, ALU.is_equal, WP, ALU.mult)
    ts(YG, QC, 1.0, ALU.is_equal, WP, ALU.mult)
    ts(T0, E(10), -1310720.0, ALU.mult)
    ts(LCW, YL, 1184.0, ALU.mult, T0, ALU.add)
    affine(LCM, BON, LCW)
    cp(A("wtf"), A("wti"))
    affine(WU, UT, C("wtf", 0))
    affine(WV, UT, C("wtf", 1))
    ts(T1, P3, 0.0, ALU.is_equal, C("rm", 10), ALU.mult)
    ts(VBI, T1, -192.0, ALU.mult, E(10), ALU.add)
    ts(T2, P3, 1.0, ALU.is_equal, C("rm", 10), ALU.mult)
    ts(B0, T2, 6144.0, ALU.mult, VBI, ALU.add)
    ts(A8("qnh", 0, 256), A8("qni", 0, 256), 1.0 / 32, ALU.mult, 191.515625, ALU.add)
    cp(A8("qnf", 0, 256), A8("qni", 0, 256))
    pe((A("ps4", 0, 256), [(A8("g8", 0, 128), A8("qnh", 0, 256)), (A8("g8", 128, 256), A8("qnf", 0, 256))]))
    affine(A("bw0", 768, 1024), A("ps4", 0, 256), C("rm", 10), B0)
    act(A("bw0", 512, 768), A("bw0", 0, 256), ACT.Copy)
    ms(A("bw0", 256, 512), 16.0)
    for mi in range(7):
        affine(M(mi, "f1"), IDM, C("rm", 8 + mi))
        ts(M(mi, "f2"), JM, C("rm", 6 - mi), ALU.mult)
    for lo, hi, bank in ((0, 512, "ps2"), (512, 896, "ps5")):
        pe((A(bank, 0, hi - lo), [(IDM, A("f1", lo, hi)), (IDM, A("f2", lo, hi))]))
        affine(A("f3", lo, hi), A(bank, 0, hi - lo), -1.0)
    ts(G7, PF, PC, ALU.subtract, 7.0, ALU.add)
    ts(A("tg", 0, 9), A("io16", 0, 9), 2.0, ALU.mult)
    tt(A("tg", 0, 9), A("tg", 0, 9), A("rm", 7, 16), ALU.mult)
    ts(A("tg", 16, 25), A("io16", 0, 9), -1.0, ALU.mult, G7, ALU.add)
    tt(A("tg", 0, 9), A("tg", 0, 9), A("tg", 16, 25), ALU.add)
    for mi in range(9):
        ts(M(mi, "f4"), A("xio"), C("tg", mi), ALU.is_equal, C("rm", 7 if mi == 0 else 15), ALU.mult)
    nd_ = CFG["nd"]
    direct = [m for j in range(nd_) for m in (9 + j, 7 - j)]
    ts(A("tg", 16, 32), io, G7, ALU.add, -7.0, ALU.add)
    for j, m in enumerate(direct):
        ts(M(j, "f6"), A("xio"), C("tg", 15 + m), ALU.is_equal, C("rm", m - 1), ALU.mult)
    ts(THR, PC, 0.25, ALU.mult, 0.25, ALU.add)
    affine(SFX, LT, -63.0)
    affine(PEN, LT, -8192.0)
    asel(PEN, PEN, [[1, 128]], ALU.not_equal, 8192.0, 0, -1)
    iota(A("junk", 0, LB), [[0, LB // 16], [1, 16]], 0, 0)
    ts(A("dbig", 0, LB), A("junk", 0, LB), PC, ALU.is_equal, 65536.0, ALU.mult)
    ts(A("dbig", LB, 2 * LB), A("junk", 0, LB), PC, ALU.not_equal, 65536.0, ALU.mult)
    row(K1R, Z, 2, 1.0)
    row(Q16, Z, 11, -16.0)
    row(DM, Z, 12, -32.0)
    row(DM, DM, 13, 16.0)
    row(K3R, Z, 4, 1.0)
    row(R15, Z, 15, 1.0)
    row(X16, Z, 12, 16.0)
    ms(A("pt5"), 0.0)
    tt(P5(0, 0, 2), E(4, 2), E(6, 2), ALU.add)
    tt(P5(0, 4, 6), E(4, 2), E(6, 2), ALU.add)
    cp(P5(0, 8, 10), E(8, 2))
    cp(P5(0, 13, 14), E(12))
    ts(P5(0, 11, 12), E(12), -1.0, ALU.mult)
    cp(P5(1, 11, 12), E(2))
    ts(A("col", C32, C32 + 2), E(2, 2), 32.0, ALU.mult)
    ts(A("col", CM32, CM32 + 2), E(2, 2), -32.0, ALU.mult)
    ts(P5(1, 0, 2), E(0, 2), 0.0, ALU.mult, C("col", C32), ALU.add)
    ts(P5(1, 2, 4), E(0, 2), C("col", CM32), ALU.add)
    ts(P5(1, 4, 6), E(0, 2), 0.0, ALU.mult, C("col", CM32 + 1), ALU.add)
    ts(P5(1, 6, 8), E(0, 2), C("col", C32 + 1), ALU.add)
    tt(P5(1, 12, 13), E(2), E(3), ALU.add)
    for j in (0, 4, 8):
        cp(P5(2, j, j + 2), E(0, 2))
        cp(P5(3, j, j + (3 if j == 8 else 2)), E(8, 3 if j == 8 else 2))
    for gi in range(8):
        affine(A("f5", gi * 64, gi * 64 + 64), A("pt5"), C("gm", gi))
    prev = E(10)
    for n, (r, wv) in enumerate([(0, -32.0), (1, -32.0), (2, -192.0), (6, -224.0), (7, -32.0)]):
        dst = SBI if n == 4 else C("col", 26 + n)
        ts(dst, E(r), wv, ALU.mult, prev, ALU.add)
        prev = dst
    for k in range(8):
        lo, hi = TB + 512 * k, TB + 512 * k + 512
        bank = A("ps%d" % (0, 1, 3, 6, 7)[k % 5])
        ts(A("zt", lo, hi), A("ft", lo, hi), 0.0625, ALU.mult, 191.53125, ALU.add)
        pe((bank, [(IDM, A("ft", lo, hi)), (N16, A("zt", lo, hi))]))
        affine(A("kt", lo, hi), bank, 1.0, 3072.0)
    ms(A("zt", 0, TB), 192.0)
    ts(A("ft", 0, TB), io, 0.0, ALU.mult, E(2), ALU.add)
    ts(A("fc", 0, 256), A("nkc"), 1.0 / 128, ALU.mult, 191.50390625, ALU.add)
    ts(A("nki", 0, 256), A("nkc"), 2, ALU.arith_shift_right, 31, ALU.bitwise_and)
    cp(A("fc", 256, 512), A("nki", 0, 256))
    ts(A("nki", 256, 512), A("nkc"), 3, ALU.bitwise_and)
    for k in range(1, 4):
        ts(A("fc", 256 + 256 * k, 512 + 256 * k), A("nki", 256, 512), float(k), ALU.is_equal)
    for r in range(5):
        dma("y", A("ft", TB, TB + W, 1, r, 128, 16), A("fc", 256 * r, 256 * r + 256), 65536 * (r + 1))
    asel(A("st4"), A("zero"), [[-256, 9], [1, 16]], ALU.not_equal, 1.0, -79, 16)
    asel(A("st15"), A("zero"), [[-256, 9], [1, 16]], ALU.not_equal, 1.0, -255, 16)
    ts(PH, PC, 0.5, ALU.add)
    ts(A("kb", 0, 6), A("io16", 0, 6), 16.0, ALU.mult, PH, ALU.add)
    for t in range(4):
        affine(A("lt4", 16 * t, 16 * t + 16), io, 16.0, PC)
    iota(A("dmy"), [[0, 4], [16, 4]], TB + W, 0)
    ts(A("dmy"), A("dmy"), PC, ALU.add)
    iota(A("junk2"), [[1, 16], [0, 16]], 0, 0)
    ts(A("tri"), A("junk2"), PC, ALU.is_gt)
    ts(A("yw", 0, 8), A("gm"), YL, ALU.mult)
    ts(A("yw", 8, 16), A("gm"), YG, ALU.mult)
    ms(A("ob", 32, 48), 0.0)
    ms(A("bw0", 1792, 2048), 16.0)
    nchunk = [0]

    def step(t, s, b):
        bw = "bw%d" % t
        c0, c1 = LB * b, LB * b + LB
        pin = A(bw, c0, c1) if s % 2 == 0 else A("pb", c0, c1)
        pout = A("pb", c0, c1) if s % 2 == 0 else A(bw, c0, c1)
        dd, stile = A(bw, 256 + c0, 256 + c1), A(bw, 768 + c0, 768 + c1)
        hsb = "hs0" if (t, s) == (0, 0) else "hs"

        def L(name):
            return A(name, c0, c1)

        def R(k, bank="ps%d" % (2 + b)):
            return A(bank, k * LB, (k + 1) * LB)
        pe((R(0), [(WU, pin)]), (R(1), [(WV, pin)]), (R(2), [(LCM, stile)]))
        cp(L("usb"), R(0))
        tt(L("tt"), L("usb"), R(1), ALU.mult)
        tt(L("xi"), L("tt"), R(2), ALU.add)
        ts(L("hi"), L("xi"), 5, ALU.arith_shift_right, W - 1, ALU.bitwise_and)
        cp(L("off"), L("hi"))
        ts(L(hsb), L("off"), -2048.0, ALU.add)
        n = nchunk[0]
        nchunk[0] += 1
        kg, nq = "kg%d" % (n % NKG), "nq%d" % (n % NNQ)
        vg = CFG["vg"].get((s, b), 0)
        copy("s", A(kg, 0, 16 * (LB - vg)), IND(A("kt", TB, TB + W), A("off", c0, c1 - vg)))
        if vg:
            copy("v", A(kg, 16 * (LB - vg), 16 * LB), IND(A("kt", TB, TB + W), A("off", c1 - vg, c1)))

        def key(m):
            return A(kg, m - 1, 16 * LB, 16)

        def block(mi, bank):
            return (R(mi, bank), [(M(mi, "f3"), pin), (M(mi, "f1"), key(9 + mi)), (M(mi, "f2"), key(7 - mi))])
        na, pc = CFG["na"], CFG["pc"]
        pe((R(7, "ps0"), [(IDM, pin)]))
        for mi in range(nd_, na, pc):
            pe(*[block(j, "ps0") for j in range(mi, min(na, mi + pc))])
        for mi in range(na, 7, pc):
            pe(*[block(j, "ps1") for j in range(mi, min(7, mi + pc))])

        def slot(j):
            return R(1 + j if j < nd_ else 9 + j - nd_, nq)
        for j, m in enumerate(direct):
            tt(slot(j), key(m), R(7, "ps0"), ALU.not_equal)
        ts(A(nq, (nd_ + 1) * LB, (na + 1) * LB), A("ps0", nd_ * LB, na * LB), 0.0, ALU.not_equal)
        tt(R(0, nq), key(8), R(7, "ps0"), ALU.not_equal)
        tt(R(8, nq), key(16), R(7, "ps0"), ALU.not_equal)
        ts(A(nq, (na + 1) * LB, 8 * LB), A("ps1", na * LB, 7 * LB), 0.0, ALU.not_equal)
        pe((R(0), [(M(mi, "f4"), R(mi, nq)) for mi in list(range(nd_ + 1, na + 1)) + [0, 8]]
            + [(M(j, "f6"), slot(j)) for j in range(2 * nd_)]), stop=False)
        pe((R(0), [(M(mi, "f4"), R(mi, nq)) for mi in range(na + 1, 8)]), start=False)
        ts(L("mat"), R(0), THR, ALU.is_le)
        pe((R(1), [(IDM, L(hsb)), (PEN, L("mat"))]), (R(2), [(SFX, L("mat"))]))
        ts(L("ohh"), R(1), -8192.0, ALU.add, -2050.0, ALU.max)
        ts(L("mm"), R(2), 255.0, ALU.add, 192.0, ALU.max)
        pe((R(3), [(IDM, A("dbig", LB, 2 * LB)), (BON, L("ohh"))]))
        scan(L("sc"), A("dbig", 0, LB), R(3), 0.0, ALU.add, ALU.min)
        o2 = A("off2", 16 * s + c0 // 16, 16 * s + c1 // 16)
        ts(o2, A("sc", c0 + 15, c1, 16), 32814.0, ALU.add)
        fg = A("fg", 256 * s + c0, 256 * s + c1)
        cp(fg, IND(A("ft", 0, TB + W), o2))
        tt(L("tz"), IND(A("zt", 0, TB + W), o2), L("mm"), ALU.subtract)
        pe((R(0), [(K1R, fg)]), (R(2), [(SM, stile), (FM, fg)]))
        if s == ST - 1:
            pe((R(4), [(K3R, A("fg", 256 * j + c0, 256 * j + c1)) for j in range(ST)]))
            act(L("ncb"), R(4), ACT.Relu, 1.0, -1.0)
            scan(A("ncb", 256 + c0, 256 + c1), L("ncb"), L("ncb"), C("ncb", 255 + c0) if b else 0.0, ALU.add, ALU.max)
        tt(L("eb"), R(0), dd, ALU.mult)
        ts(stile, R(2), SBI, ALU.add, 0.0, ALU.max)
        pe((R(1), [(IDM, pin), (SFX, L("mat")), (IDM, L("eb")), (Q16, stile)]))
        tt(pout, R(1), L("tz"), ALU.max)
        pd = R(0, "ps%d" % (6 + b % 2))
        pe((pd, [(IDM, pin), (IDM, dd), (DM, stile), (NID, pout)]))
        if en(("d16", s)) == "s":
            act(dd, pd, ACT.Relu)
        else:
            ts(dd, pd, 0.0, ALU.max)
        if (t, s) == (RO - 1, ST - 1):
            pe((R(5), [(IDM, pout), (X16, stile), (IDM, dd)]))
            affine(A(bw, 1792 + c0, 1792 + c1), R(5), 1.0, -16.0)

    def finish(t):
        bw, snd = "bw%d" % t, "snd%d" % t
        last = t == RO - 1
        tiles = [0, 1, 3] if last else [0, 1, 2, 3]
        nt = len(tiles)
        own = [0, 1792 if last else 256, 512, 768]
        valued = [1024, 1024 if last else 1792, 1024, 1280]
        spare = [512, 512 if last else 1792, 512, 1536]
        ts(A("cout%d" % t), A("ncb", 504, 512), float(CAP), ALU.min, 4096.0, ALU.mult)
        send(t, 2 * t, A("cout%d" % t), A("cin%d" % t), 2500.0 if last else 4500.0)
        for c in range(6):
            act(A("junk", 0, 192), A("ncb", 256, 448), ACT.Sign, C("kb", c), -1.0, C("cn", c))
        ts(A("cn", 0, 4), A("cn", 0, 4), 256.0, ALU.add)
        ts(A("cn", 4, 6), A("cn", 4, 6), 192.0, ALU.add)
        for c in range(4):
            act(A("junk", 192, 256), A("ncb", 448, 512), ACT.Sign, C("kb", c), -1.0, C("cn", 8 + c))
        for c in range(4, 6):
            j2 = A("junk2", 64 * (c - 4), 64 * (c - 3))
            ts(j2, A("ncb", 448, 512), C("kb", c), ALU.is_le, 2.0, ALU.mult)
            add("v", "red", (C("cn", 8 + c), j2), [C("cn", 8 + c)], [j2], 64.0)
        tt(A("cn", 16, 22), A("cn", 0, 6), A("cn", 8, 14), ALU.add)
        ts(A("lst", 0, 6), A("cn", 16, 22), 0.5, ALU.mult, 255.0, ALU.min)
        for n, tl in enumerate(tiles):
            copy(en(("snd", t, tl), "s" if tl in (1, 2) else "v"), A(snd, CAP * n, CAP * n + CAP), IND(A(bw, own[tl], own[tl] + 256), A("lst", 0, 6)))
        send(t, 2 * t + 1, A(snd, 0, CAP * nt), A(bw, ARR, ARR + CAP * nt), 3000.0 if last else 5000.0)
        to_t(A("ps0", 0, 64), "st4", "fg", 0, 1024)
        for s in range(ST):
            ts(A("atw", 16 * s, 16 * s + 16), A("off2", 16 * s, 16 * s + 16), 8192.0 * (ST - s), ALU.add)
        tt(A("cod"), A("ps0", 0, 64), A("atw"), ALU.mult)
        tt(A("cod2"), A("cod", 0, 32), A("cod", 32, 64), ALU.max)
        tt(A("codi", 0, 16), A("cod2", 0, 16), A("cod2", 16, 32), ALU.max)
        ts(A("codi", 16, 32), A("codi", 0, 16), 8191, ALU.bitwise_and)
        cp(A("atv"), A("codi", 16, 32))
        affine(A("zz"), IND(A("zt", 0, TB + W), A("atv")), 1.0, -192.0)
        act(A("fv"), IND(A("ft", 0, TB + W), A("atv")), ACT.Copy)
        pe((A("ps3", 0, 256), [(IDM, A(bw, 512, 768)), (IDM, A("zz"))]))
        ts(A("tb"), A("ps3", 0, 256), 16.0, ALU.is_ge, -16.0, ALU.mult)
        if last:
            tt(A(bw, 1024, 1280), A("ps3", 0, 256), A("tb"), ALU.add)
        else:
            pe((A("ps3", 256, 512), [(IDM, A(bw, 512, 768)), (IDM, A("zz")), (IDM, A("tb"))]))
            act(A(bw, 1024, 1280), A("ps3", 256, 512), ACT.Copy)
        pe((A("ps4", 0, 256), [(VM, A("fv"))]), (A("ps4", 256, 512), [(FFM, A(bw, 768, 1024))]))
        affine(A(bw, 1280, 1536), A("ps4", 0, 256), 1.0, VBI)
        act(A(bw, 1536, 1792), A("ps4", 256, 512), ACT.Copy)
        to_t(A("ps2", 0, 32), "st4", "ncb", 0, 512)
        cp(A("nct"), A("ps2", 0, 32))
        nd, cu = A("nct", 0, 16), A("nct", 16, 32)
        if not last:
            affine(A("zraw"), A("zz"), 1.0, 192.0)
            ts(A("so1"), nd, 10000.0, ALU.mult)
            tt(A("pls"), A("plt"), A("so1"), ALU.add)

            def eq(c):
                return A("eqb", c, 16 * (63 - 16 * (c % 4)) + c + 1, 16)
            for c in range(16):
                ts(eq(c), A("prow", 16 * c, 64 * (c // 4) + 64), C("pls", c), ALU.is_equal)
                ops[-1]["wr"] = [("eqc", c, c + 1)]
            tt(A("eqb", 0, 256), A("eqb", 0, 256), A("tri"), ALU.mult)
            ops[-1]["rd"] = ops[-1]["rd"] + [("eqc", 0, 16)]
            pe(*[(A("ps6", 64 * k, 64 * k + 64), [(IDM, A("ncb", 64 * k, 64 * k + 64))]
                  + [(A("ps6", 16 * c, 64 * k + 64), BON, eq(c)) for c in range(4 * k + 3, 4 * k - 1, -1)]) for k in range(4)])
            ts(A("win"), A("ps6", 0, 256), 0.0, ALU.is_equal)
            to_t(A("ps7", 0, 16), "st4", "win", 0, 256)
            tt(A("so1"), A("ps7", 0, 16), A("pld"), ALU.mult)
            tt(A("so2"), A("so1"), A("dmy"), ALU.add)
            cp(A("sof"), A("so2"))
            for nm, src, lo in (("kt", bw, 512), ("ft", "fv", 0), ("zt", "zraw", 0)):
                for k in range(3, -1, -1):
                    cp(IND(A(nm), A("sof", 4 * k, 4 * k + 4)), A(src, lo + 64 * k, lo + 64 * k + 64))
        ts(A("lv"), cu, CAP + 0.5, ALU.is_le)
        tt(A("lv"), A("lv"), nd, ALU.mult)
        ts(A("cux", 0, 16), nd, -1000.0, ALU.mult, 1000.0, ALU.add)
        tt(A("cux", 16, 32), A("cux", 0, 16), cu, ALU.add)
        cux = A("cux", 16, 32)
        for n, tl in enumerate(tiles):
            sl = (16 * n, 16 * n + 16)
            affine(A("oa", *sl), nd, float(own[tl] - valued[tl]), float(valued[tl]))
            if spare[tl] != own[tl]:
                affine(A("ob", *sl), A("lv"), float(spare[tl] - own[tl]))
            affine(A("ca", *sl), cux, 1.0, ARR + CAP * n - 1.0)
            affine(A("cx", *sl), cux, -4095.0, ARR + CAP * n - 1.0)
        wd = (0, 16 * nt)
        tt(A("oa", *wd), A("oa", *wd), A("lt4", *wd), ALU.add)
        tt(A("o0", *wd), A("oa", *wd), A("ob", *wd), ALU.add)
        ts(A("aa", *wd), A("cx", *wd), C("cin%d" % t, 7), ALU.add)
        tt(A("aa", *wd), A("aa", *wd), A("ca", *wd), ALU.min)
        tt(A("ab", *wd), A("aa", *wd), A("o0", *wd), ALU.max)
        cp(A("aof", *wd), A("ab", *wd))
        win = A(bw, 0, ARR + CAP * nt)
        if not last:
            for lo, hi in ((0, 8), (48, 56), (8, 16), (56, 64), (16, 32), (32, 48)):
                copy(en(("asm", lo), "s"), A("bw1", 16 * lo, 16 * hi), IND(win, A("aof", lo, hi)))
        else:
            for lo, hi, eng in ((32, 40, "v"), (40, 48, "s"), (0, 16, "v"), (16, 32, "s")):
                copy(eng, A("outb", 16 * lo, 16 * hi), IND(win, A("aof", lo, hi)))
            dma("y", ("ext", "yp", full), A("outb", 0, 512), 131072)
            pe((A8("ps0", 0, 256), [(A("yw", 0, 8), A("outb", 512, 768))]))
            pe((A8("ps1", 0, 256), [(A("yw", 8, 16), A("outb", 512, 768))]))
            act(A8("yno", 0, 256), A8("ps0", 0, 256), ACT.Copy)
            cp(A8("yno", 256, 512), A8("ps1", 0, 256))
            dma("s", ("ext", "yn", full), A8("yno", 0, 512), 16384)

    for t in range(RO):
        for s in range(ST):
            for b in range(NB):
                step(t, s, b)
            if (t, s) == (0, 1):
                pe((A("ps6", 256, 512), [(R15, A("hs0"))]))
                cp(A("prow"), A("ps6", 256, 512))
                to_t(A("ps7", 256, 272), "st15", "hs0", 0, 256)
                cp(A("plt"), A("ps7", 256, 272))
                ts(A("so2"), A("plt"), 2048.0 + TB, ALU.add)
                tt(A("pld"), A("so2"), A("dmy"), ALU.subtract)
        finish(t)
    return ops


def depend(ops):
    hist, banks = {}, {}
    for n, op in enumerate(ops):
        deps = set()
        for name, lo, hi in op["rd"]:
            for m, a, b, w in hist.get(name, []):
                if w and a < hi and lo < b:
                    deps.add(m)
        for name, lo, hi in op["wr"]:
            for m, a, b, w in hist.get(name, []):
                if a < hi and lo < b and not (op["kind"] == "dma" and ops[m]["kind"] == "dma"):
                    deps.add(m)
        for name in set(r[0] for r in op["rd"] + op["wr"] if r[0].startswith("ps")):
            cur, prev, eng = banks.get(name, ([], [], None))
            if eng == op["eng"]:
                deps.update(prev)
                banks[name] = (cur + [n], prev, eng)
            else:
                deps.update(cur)
                banks[name] = ([n], cur, op["eng"])
        if op["kind"] == "arrive":
            deps = {op["args"][1]}
        for name, lo, hi in op["wr"]:
            if op["kind"] != "dma":
                hist[name] = [h for h in hist.get(name, []) if not (lo <= h[1] and h[2] <= hi and h[0] in deps)]
            hist.setdefault(name, []).append((n, lo, hi, True))
        for name, lo, hi in op["rd"]:
            hist.setdefault(name, []).append((n, lo, hi, False))
        deps.discard(n)
        op["deps"] = sorted(deps)


def schedule(ops):
    n = len(ops)
    users = [[] for _ in range(n)]
    for k, op in enumerate(ops):
        for d in op["deps"]:
            users[d].append(k)
    rest = [0.0] * n
    nxt = 0.0
    for k in range(n - 1, -1, -1):
        rest[k] = ops[k]["cost"] + ops[k]["lat"] + max([CFG["hop"] + rest[u] for u in users[k]] + [0.0])
        if ops[k]["eng"] == "s" and any(w[0].startswith("kg") for w in ops[k]["wr"]):
            rest[k] = nxt = max(rest[k], nxt + CFG["pace"] * ops[k]["cost"])
    left = [len(op["deps"]) for op in ops]
    ready = {k: 0.0 for k in range(n) if left[k] == 0}
    free, order, end = {}, [], [0.0] * n
    while ready:
        start = {k: max(r, free.get(ops[k]["eng"], 0.0)) for k, r in ready.items()}
        first = min(start, key=lambda k: (start[k], -rest[k]))
        eng = ops[first]["eng"]
        k = max((j for j in start if ops[j]["eng"] == eng and start[j] <= start[first] + CFG["slack"]), key=lambda j: (rest[j], -j))
        del ready[k]
        free[eng] = start[k] + ops[k]["cost"]
        end[k] = free[eng] + ops[k]["lat"]
        ops[k]["start"] = start[k]
        order.append(k)
        for u in users[k]:
            left[u] -= 1
            if left[u] == 0:
                ready[u] = max(end[d] + (CFG["self"] if ops[d]["eng"] == ops[u]["eng"] else CFG["hop"]) for d in ops[u]["deps"])
    return order, max(end)


def plan():
    ops = build_ops()
    depend(ops)
    order, total = schedule(ops)
    count, clock = {}, {}
    for k in order:
        op = ops[k]
        eng, kind = op["eng"], op["kind"]
        ck = clock.setdefault(eng, {})
        waits = {}
        if kind != "arrive":
            for d in sorted(op["deps"], key=lambda j: -ops[j]["start"]):
                sem, val = ops[d]["tok"]
                if ck.get(sem, 0) < val:
                    waits[sem] = max(waits.get(sem, 0), val)
                    for s2, v2 in ops[d]["clock"].items():
                        ck[s2] = max(ck.get(s2, 0), v2)
        op["waits"] = sorted(waits.items())
        if kind == "dma":
            tok = ("d%d" % op["args"][2], 16)
        elif kind == "arrive":
            tok = ("ar%d" % op["args"][0], 1)
        elif kind == "send":
            tok = ("ls", 1)
        else:
            sem = "s" + eng
            count[sem] = count.get(sem, 0) + (len(op["args"]) if kind == "mm" else 1)
            tok = (sem, count[sem])
        op["tok"] = tok
        op["clock"] = {} if kind == "arrive" else dict(ck)
        op["clock"][tok[0]] = tok[1]
    return ops, order, total, count


PLAN = []


def route(T, topo, t, r):
    n = len(T.cores)
    src, dst = T.cores[r], T.cores[(r + 1 + t) % n]
    if topo.may_write(src, dst):
        return dst, None, topo.mask(src, dst)
    able = [c for c in topo.cores_of(src) if c != src and topo.may_write(c, dst)]
    able.sort(key=lambda c: (topo.die(c) != topo.die(src), c))
    return dst, able[0], topo.mask(src, able[0]) & topo.mask(able[0], dst)


def engines_in(mask):
    return bin(mask).count("1")


def rank_program(g, core, T, topo):
    if not PLAN:
        PLAN.append(plan())
    ops, order, total, count = PLAN[0]
    n = len(T.cores)
    rank = T.rank_of(core)
    sent = 0
    if rank is None:
        for k in order:
            if ops[k]["kind"] == "send":
                t, m, src, land = ops[k]["args"]
                for r in range(n):
                    dst, via, mask = route(T, topo, t, r)
                    if via == core:
                        g.wait_ge(T.sem["ar%d" % m], engines_in(mask))
                        rid, pid = topo.addr(dst, core)
                        g.remote_dma(real(T, land), real(T, land), T.sem["ar%d" % m], T.sem.hl, pid, rid, mask)
                        sent += engines_in(mask)
        if sent:
            g.wait_ge(T.sem.hl, sent)
        return
    arrive = [engines_in(route(T, topo, t, (rank - 1 - t) % n)[2]) for t in range(RO)]
    queue = {"v": g.vector, "s": g.scalar, "p": g.tensor, "g": g, "y": g.sync}
    for k in order:
        op = ops[k]
        kind, a = op["kind"], op["args"]
        if kind == "arrive":
            continue
        q = queue[op["eng"]]
        for sem, val in op["waits"]:
            q.wait_ge(T.sem[sem], arrive[int(sem[2]) // 2] if sem.startswith("ar") else val)
        sem = T.sem[op["tok"][0]]
        if kind == "mm":
            for terms in a:
                for j, (o, l, rr) in enumerate(terms):
                    ins = q.matmul(real(T, o), real(T, l), real(T, rr), j == 0 and op["ends"][0], j == len(terms) - 1 and op["ends"][1])
                ins.then_inc(sem, 1)
            continue
        r = [real(T, x) for x in a]
        if kind == "send":
            dst, via, mask = route(T, topo, a[0], rank)
            rid, pid = topo.addr(dst if via is None else via, core)
            g.remote_dma(r[3], r[2], T.sem["ar%d" % a[1]], sem, pid, rid, mask)
            sent += engines_in(mask)
        elif kind == "dma":
            q.dma_start(r[0], r[1]).then_inc(sem, 16)
        elif kind == "ts":
            if a[5] is None:
                q.tensor_scalar(r[0], r[1], r[2], None, r[4]).then_inc(sem, 1)
            else:
                q.tensor_scalar(r[0], r[1], r[2], r[3], r[4], r[5]).then_inc(sem, 1)
        elif kind == "tt":
            q.tensor_tensor(r[0], r[1], r[2], r[3]).then_inc(sem, 1)
        elif kind == "cp":
            q.tensor_copy(r[0], r[1]).then_inc(sem, 1)
        elif kind == "ms":
            q.memset(r[0], r[1]).then_inc(sem, 1)
        elif kind == "scan":
            q.tensor_tensor_scan(r[0], r[1], r[2], r[3], r[4], r[5]).then_inc(sem, 1)
        elif kind == "red":
            q.tensor_reduce(r[0], r[1], AxisListType.X, ALU.add).then_inc(sem, 1)
        elif kind == "act":
            q.activation(r[0], r[1], r[2], bias=r[3], scale=r[4], accum_out=r[5]).then_inc(sem, 1)
        elif kind == "iota":
            if SB[a[0][1]][1] == I32:
                q.iota(r[0], r[1], r[2], r[3]).then_inc(sem, 1)
            else:
                q.iota(r[0], r[1], r[2], r[3], allow_small_or_imprecise_dtypes=True).then_inc(sem, 1)
        elif kind == "asel":
            q.affine_select(r[0], r[1], r[2], r[3], r[4], r[5], r[6]).then_inc(sem, 1)
    for op in ops:
        if op["kind"] == "dma":
            g.sync.wait_ge(T.sem[op["tok"][0]], 16)
    for sem, val in sorted(count.items()):
        g.sync.wait_ge(T.sem[sem], val)
    g.wait_ge(T.sem.ls, sent)
